import numpy as np
import ml_dtypes


def mxq(x, axis, fmt="e4m3"):
    dtype, down = {"e4m3": (ml_dtypes.float8_e4m3fn, 7), "e5m2": (ml_dtypes.float8_e5m2, 14)}[fmt]
    v = np.moveaxis(np.asarray(x, np.float32).astype(ml_dtypes.bfloat16).astype(np.float64), axis, -1)
    blocks = v.reshape(v.shape[:-1] + (-1, 32))
    amax = np.abs(blocks).max(-1, keepdims=True)
    byte = np.maximum(np.where(amax > 0, np.frexp(amax)[1] - 1 + 127, 0) - down, 1)
    scale = np.exp2(byte - 127.0)
    codes = (blocks / scale).astype(np.float32).astype(dtype).astype(np.float64)
    return np.moveaxis((codes * scale).reshape(v.shape), -1, axis)


WIDE = False


def mx_kscale(k):
    if not WIDE:
        return np.ones(k)
    levels = np.array([10, -10, 5, -5, 0])
    if k % 512:
        return np.exp2(np.random.permutation(np.resize(levels, k // 32))).repeat(32)
    a = np.empty((k // 512, 16))
    for p in range(k // 512):
        a[p, :8] = np.random.permutation(np.resize(levels, 8))
        for g in range(8):
            far = levels[np.abs(levels - a[p, g]) >= 10]
            a[p, g + 8] = far[np.random.randint(len(far))]
    return np.exp2(a.ravel()).repeat(32)


def f64(x):
    return np.asarray(x).astype(np.float64)


def striped(idx):
    return np.tile(idx.reshape(-1, 16).T, (8, 1)).astype(np.uint16)


def unstriped(offs):
    return offs[:16].T.reshape(-1).astype(np.int64)


def pack_weight(w):
    k, n = w.shape
    w = f64(np.asarray(w, np.float32).astype(ml_dtypes.bfloat16)).reshape(k // 32, 32, n)
    amax = np.abs(w).max(1)
    byte = np.clip(np.where(amax > 0, np.frexp(amax)[1] - 1 + 127 - 7, 1), 1, 254)
    scaled = (w * np.exp2(127.0 - byte)[:, None, :]).reshape(k, n).astype(np.float32)
    words = np.ascontiguousarray(scaled.reshape(k // 512, 128, 4, n).transpose(0, 1, 3, 2)).astype(ml_dtypes.float8_e4m3fn).view(np.uint8)
    return words, np.ascontiguousarray(byte.astype(np.uint8).reshape(k // 512, 16, n))


def unpack_weight(words, scales):
    g, p, n, _ = words.shape
    vals = np.ascontiguousarray(words).view(ml_dtypes.float8_e4m3fn).astype(np.float64) * np.repeat(np.exp2(scales.astype(np.float64) - 127.0), 8, axis=1)[..., None]
    return vals.transpose(0, 1, 3, 2).reshape(g * 512, n)


E2M1 = np.array([0.0, 0.5, 1.0, 1.5, 2.0, 3.0, 4.0, 6.0, -0.0, -0.5, -1.0, -1.5, -2.0, -3.0, -4.0, -6.0])


def pack_fp4(w):
    k, n = w.shape
    w = f64(np.asarray(w, np.float32).astype(ml_dtypes.bfloat16)).reshape(k // 32, 32, n)
    amax = np.abs(w).max(1)
    mant, ex = np.frexp(amax / 6.0)
    byte = np.clip(np.where(amax > 0, np.where(mant > 0.5, ex, ex - 1) + 127, 1), 1, 254)
    scaled = (w * np.exp2(127.0 - byte)[:, None, :]).reshape(k, n).astype(np.float32)
    c = np.ascontiguousarray(scaled.reshape(k // 512, 128, 4, n).transpose(0, 1, 3, 2)).astype(ml_dtypes.float4_e2m1fn).view(np.uint8) & 0xF
    words = (c[..., 0::2] | (c[..., 1::2] << 4)).reshape(k // 512, 128, 2 * n)
    return np.ascontiguousarray(words), np.ascontiguousarray(byte.astype(np.uint8).reshape(k // 512, 16, n))


def unpack_fp4(words, scales):
    g, _, n = scales.shape
    words = np.ascontiguousarray(words).reshape(g, 128, n, 2)
    nib = np.empty((g, 128, n, 4), np.uint8)
    nib[..., 0::2] = words & 0xF
    nib[..., 1::2] = words >> 4
    vals = E2M1[nib] * np.repeat(np.exp2(scales.astype(np.float64) - 127.0), 8, axis=1)[..., None]
    return vals.transpose(0, 1, 3, 2).reshape(g * 512, n)


def relu(v):
    return np.maximum(v, 0.0)


K, T, S, D, V, H, N = 1024, 4096, 1024, 2, 512, 512, 128
P = 2 ** 7


def setup_inputs():
    n = np.random.standard_normal
    s = mx_kscale(K)[:, None]
    u = mx_kscale(H)
    packed_xT = pack_weight(n((K, T)) * s)
    packed_w2 = pack_fp4(n((H, N)) / np.sqrt(H) / u[:, None])
    return {
        "x_words": packed_xT[0],
        "x_scales": packed_xT[1],
        "w1": (n((K, H)) / np.sqrt(K) / s * u).astype(np.float32),
        "w2_words": packed_w2[0],
        "w2_scales": packed_w2[1],
        "gate": (np.tile(np.random.uniform(0.2, 1.0, (D, 1, V)), (1, P, 1))).astype(np.float32),
        "offs": striped(np.random.permutation(T)[:S]),
    }


def reference(x_words, x_scales, w1, w2_words, w2_scales, gate, offs):
    xq = unpack_weight(x_words, x_scales)[:, unstriped(offs)]
    w1q = mxq(f64(w1), 0, "e4m3")
    y0 = w1q.T @ xq[:, :V]
    y1 = w1q.T @ xq[:, V:2 * V]
    z = relu(y0 * f64(gate)[0, :1] + y1 * f64(gate)[1, :1])
    return unpack_fp4(w2_words, w2_scales).T @ mxq(z, 0, "e4m3")

@@ -1,0 +1,166 @@
+from contextlib import ExitStack
+
+import concourse.mybir as mybir
+from concourse.masks import make_identity
+
+K, T, S, D, V, H, N = 1024, 4096, 1024, 2, 512, 512, 128
+FLOPS = 2 * K * H * S + 2 * H * N * V
+BYTES = K * T + K * T // 32 + 4 * K * H + H * N // 2 + H * N // 32 + 4 * D * V + 2 * 128 * S // 16 + 4 * N * V
+
+F32 = mybir.dt.float32
+BF16 = mybir.dt.bfloat16
+I32 = mybir.dt.int32
+U32 = mybir.dt.uint32
+U16 = mybir.dt.uint16
+U8 = mybir.dt.uint8
+FP8X4 = mybir.dt.float8_e4m3fn_x4
+FP4X4 = mybir.dt.float4_e2m1fn_x4
+ACT = mybir.ActivationFunctionType
+ALU = mybir.AluOpType
+
+P = 128
+PACK = 4
+PASSES = K // (P * PACK)
+BLOCKS = V // P
+
+
+def tile_picked_zbloom_relu_p_kernel(
+    tc, x_words, x_scales, w1, w2_words, w2_scales, gate, offs, out
+):
+    nc = tc.nc
+    with ExitStack() as ctx:
+        keep = ctx.enter_context(tc.tile_pool(name="keep", bufs=1))
+        psum = ctx.enter_context(tc.psum_pool(name="psum", bufs=1))
+
+        offsets = keep.tile([P, S // 16], U16, name="offsets")
+        nc.sync.dma_start(offsets[:], offs)
+
+        table_scales = keep.tile([P, T], U8, name="table_scales", tag="scales_then_words", align_bytes=64)
+        nc.sync.dma_start(
+            table_scales[96:P, :].bitcast(I32), x_scales.rearrange("o q n -> (o q) n").bitcast(I32)
+        )
+        nc.vector.memset(table_scales[0:96, :].bitcast(I32), 0)
+
+        gate_rows = keep.tile([P, P], F32, name="gate_rows")
+        nc.sync.dma_start(
+            gate_rows[P - D * BLOCKS : P, :], gate[:, 0, :].rearrange("d (b p) -> d b p", p=P)
+        )
+        nc.vector.memset(gate_rows[0:96, :], 0.0)
+        nc.vector.memset(gate_rows[96 : P - D * BLOCKS, :], 0.0)
+        w2_codes = keep.tile([P, 2 * N], U8, name="w2_codes", align_bytes=64)
+        nc.sync.dma_start(w2_codes[:].bitcast(I32), w2_words[0].bitcast(I32))
+
+        w1_raw = []
+        for o in range(PASSES):
+            raw = keep.tile([P, PACK, H], F32, name=f"w1_raw{o}")
+            nc.sync.dma_start(raw[:], w1[512 * o : 512 * (o + 1), :].rearrange("(p j) c -> p j c", j=PACK))
+            w1_raw.append(raw)
+
+        def load_words(o, tag):
+            words = keep.tile([P, T], I32, name=f"table_words{o}", tag=tag, align_bytes=64)
+            nc.sync.dma_start(words[:], x_words[o].rearrange("p n t -> p (n t)").bitcast(I32))
+            return words
+
+        table_words = [load_words(0, "words")]
+
+        identity = keep.tile([P, P], F32, name="identity")
+        make_identity(nc, identity[:])
+
+        gate_turned = psum.tile([P, P], F32, name="gate_turned", tag="bank0_0")
+        nc.tensor.transpose(gate_turned[:], gate_rows[:], identity[:])
+        gate_cols = keep.tile([P, D * BLOCKS], F32, name="gate_cols")
+        nc.scalar.activation(gate_cols[:], gate_turned[:, P - D * BLOCKS : P], ACT.Copy)
+
+        gathered_scales = keep.tile([P, S], U8, name="gathered_scales", align_bytes=64)
+        nc.vector.tensor_copy(gathered_scales[:], table_scales[:].indirect(offsets[:]))
+
+        def place_scales(o):
+            plane = keep.tile([P, S], U8, name=f"picked_plane{o}", align_bytes=64)
+            nc.vector.memset(plane[:].bitcast(I32), 0)
+            for q in range(4):
+                row = 96 + 16 * o + 4 * q
+                nc.sync.dma_start(
+                    plane[32 * q : 32 * q + 4, :].bitcast(I32),
+                    gathered_scales[row : row + 4, :].bitcast(I32),
+                )
+            return plane
+
+        picked_planes = [place_scales(0)]
+        table_words.append(load_words(1, "scales_then_words"))
+        picked_planes.append(place_scales(1))
+
+        w1_codes, w1_planes = [], []
+        for o in range(PASSES):
+            grouped = keep.tile([P, H * PACK], BF16, name=f"w1_grouped{o}", tag=f"grouped{o}", align_bytes=64)
+            nc.scalar.copy(
+                grouped[:].rearrange("p (u m e j) -> p m j u e", u=2, e=2, j=PACK),
+                w1_raw[o][:].rearrange("p j (m u e) -> p m j u e", u=2, e=2),
+            )
+            codes = keep.tile([P, H], U32, name=f"w1_codes{o}", align_bytes=64)
+            plane = keep.tile([P, H], U8, name=f"w1_plane{o}", align_bytes=64)
+            nc.vector.quantize_mx(codes[:].bitcast(FP8X4), plane[:], grouped[:])
+            w1_codes.append(codes)
+            w1_planes.append(plane)
+
+        w2_plane = keep.tile([P, N], U8, name="w2_plane", tag="grouped1", align_bytes=64)
+        nc.vector.memset(w2_plane[:].bitcast(I32), 0)
+        for q in range(4):
+            nc.sync.dma_start(
+                w2_plane[32 * q : 32 * q + 4, :].bitcast(I32), w2_scales[0, 4 * q : 4 * q + 4, :].bitcast(I32)
+            )
+
+        y = [[psum.tile([P, H], F32, name=f"y{d}_{b}", tag=f"bank{d}_{b}") for b in range(BLOCKS)] for d in range(D)]
+        for o in range(PASSES):
+            for d in range(D):
+                picked = keep.tile([P, V], U32, name=f"picked{o}_{d}", align_bytes=64)
+                nc.vector.tensor_copy(
+                    picked[:],
+                    table_words[o][:].bitcast(U32).indirect(offsets[:, d * V // 16 : (d + 1) * V // 16]),
+                )
+                for b in range(BLOCKS):
+                    nc.tensor.matmul_mx(
+                        y[d][b][:],
+                        lhsT=picked[:, b * P : (b + 1) * P].bitcast(FP8X4),
+                        lhsT_scale=picked_planes[o][:, d * V + b * P : d * V + (b + 1) * P],
+                        rhs=w1_codes[o][:].bitcast(FP8X4),
+                        rhs_scale=w1_planes[o][:],
+                        start=(o == 0),
+                        stop=(o == PASSES - 1),
+                    )
+
+        firsts = []
+        for b in range(BLOCKS):
+            first = keep.tile([P, H], F32, name=f"first{b}")
+            nc.scalar.activation(first[:], y[0][b][:], ACT.Copy, scale=gate_cols[:, b : b + 1])
+            firsts.append(first)
+        for b in range(BLOCKS):
+            summed = keep.tile([P, H], BF16, name=f"summed{b}", align_bytes=64)
+            nc.vector.scalar_tensor_tensor(
+                summed[:], y[1][b][:], gate_cols[:, BLOCKS + b : BLOCKS + b + 1], firsts[b][:], ALU.mult, ALU.add
+            )
+            turned = psum.tile([P, 2, P], F32, name=f"turned{b}", tag=f"bank0_{b}")
+            pairs = summed[:].bitcast(F32)
+            for u in range(2):
+                nc.tensor.transpose(turned[:, u, :], pairs[:, u * P : (u + 1) * P], identity[:])
+            z = keep.tile([P, P * PACK], BF16, name=f"z{b}", align_bytes=64)
+            nc.scalar.activation(
+                z[:].rearrange("p (v u e) -> p v u e", u=2, e=2),
+                turned[:].rearrange("p u v -> p (u v)").bitcast(BF16).rearrange("p (u v e) -> p v u e", u=2, e=2),
+                ACT.Relu,
+            )
+            z_codes = keep.tile([P, P], U32, name=f"z_codes{b}", align_bytes=64)
+            z_plane = keep.tile([P, P], U8, name=f"z_plane{b}", align_bytes=64)
+            nc.vector.quantize_mx(z_codes[:].bitcast(FP8X4), z_plane[:], z[:])
+            acc = psum.tile([N, P], F32, name=f"acc{b}", tag=f"bank1_{b}")
+            nc.tensor.matmul_mx(
+                acc[:],
+                lhsT=w2_codes[:].bitcast(FP4X4),
+                lhsT_scale=w2_plane[:],
+                rhs=z_codes[:].bitcast(FP8X4),
+                rhs_scale=z_plane[:],
+                start=True,
+                stop=True,
+            )
+            result = keep.tile([N, P], F32, name=f"result{b}")
+            nc.vector.tensor_copy(result[:], acc[:])
+            nc.sync.dma_start(out[:, b * P : (b + 1) * P], result[:])

@@ -32,15 +32,20 @@ def tile_picked_zbloom_relu_p_kernel(
         keep = ctx.enter_context(tc.tile_pool(name="keep", bufs=1))
         psum = ctx.enter_context(tc.psum_pool(name="psum", bufs=1))
 
-        offsets = keep.tile([P, S // 16], U16, name="offsets")
-        nc.sync.dma_start(offsets[:], offs)
-
-        table_scales = keep.tile([P, T], U8, name="table_scales", tag="scales_then_words", align_bytes=64)
+        table_scales = keep.tile([P, T], U8, name="table_scales", tag="scales_then_w1", align_bytes=64)
         nc.sync.dma_start(
             table_scales[96:P, :].bitcast(I32), x_scales.rearrange("o q n -> (o q) n").bitcast(I32)
         )
         nc.vector.memset(table_scales[0:96, :].bitcast(I32), 0)
 
+        def load_w1(o, tag):
+            raw = keep.tile([P, PACK, H], F32, name=f"w1_raw{o}", tag=tag, align_bytes=64)
+            nc.sync.dma_start(raw[:], w1[512 * o : 512 * (o + 1), :].rearrange("(p j) c -> p j c", j=PACK))
+            return raw
+
+        w1_raw = [load_w1(0, "w1")]
+        offsets = keep.tile([P, S // 16], U16, name="offsets")
+        nc.sync.dma_start(offsets[:], offs)
         gate_rows = keep.tile([P, P], F32, name="gate_rows")
         nc.sync.dma_start(
             gate_rows[P - D * BLOCKS : P, :], gate[:, 0, :].rearrange("d (b p) -> d b p", p=P)
@@ -49,23 +54,14 @@ def tile_picked_zbloom_relu_p_kernel(
         nc.vector.memset(gate_rows[96 : P - D * BLOCKS, :], 0.0)
         w2_codes = keep.tile([P, 2 * N], U8, name="w2_codes", align_bytes=64)
         nc.sync.dma_start(w2_codes[:].bitcast(I32), w2_words[0].bitcast(I32))
-
-        w1_raw = []
+        table_words = []
         for o in range(PASSES):
-            raw = keep.tile([P, PACK, H], F32, name=f"w1_raw{o}")
-            nc.sync.dma_start(raw[:], w1[512 * o : 512 * (o + 1), :].rearrange("(p j) c -> p j c", j=PACK))
-            w1_raw.append(raw)
-
-        def load_words(o, tag):
-            words = keep.tile([P, T], I32, name=f"table_words{o}", tag=tag, align_bytes=64)
+            words = keep.tile([P, T], I32, name=f"table_words{o}", align_bytes=64)
             nc.sync.dma_start(words[:], x_words[o].rearrange("p n t -> p (n t)").bitcast(I32))
-            return words
-
-        table_words = [load_words(0, "words")]
+            table_words.append(words)
 
         identity = keep.tile([P, P], F32, name="identity")
         make_identity(nc, identity[:])
-
         gate_turned = psum.tile([P, P], F32, name="gate_turned", tag="bank0_0")
         nc.tensor.transpose(gate_turned[:], gate_rows[:], identity[:])
         gate_cols = keep.tile([P, D * BLOCKS], F32, name="gate_cols")
@@ -86,23 +82,40 @@ def tile_picked_zbloom_relu_p_kernel(
             return plane
 
         picked_planes = [place_scales(0)]
-        table_words.append(load_words(1, "scales_then_words"))
+        w1_raw.append(load_w1(1, "scales_then_w1"))
         picked_planes.append(place_scales(1))
+
+        picked = []
+        for o in range(PASSES):
+            for d in range(D):
+                words = keep.tile([P, V], U32, name=f"picked{o}_{d}", tag=f"picked{o}_{d}", align_bytes=64)
+                nc.vector.tensor_copy(
+                    words[:],
+                    table_words[o][:].bitcast(U32).indirect(offsets[:, d * V // 16 : (d + 1) * V // 16]),
+                )
+                picked.append(words)
 
         w1_codes, w1_planes = [], []
         for o in range(PASSES):
-            grouped = keep.tile([P, H * PACK], BF16, name=f"w1_grouped{o}", tag=f"grouped{o}", align_bytes=64)
-            nc.scalar.copy(
-                grouped[:].rearrange("p (u m e j) -> p m j u e", u=2, e=2, j=PACK),
-                w1_raw[o][:].rearrange("p j (m u e) -> p m j u e", u=2, e=2),
-            )
+            grouped = keep.tile([P, H, PACK], BF16, name=f"w1_grouped{o}", tag=f"grouped{o}", align_bytes=64)
+            woven = w1_raw[o][:].rearrange("p j c -> p c j")
             codes = keep.tile([P, H], U32, name=f"w1_codes{o}", align_bytes=64)
             plane = keep.tile([P, H], U8, name=f"w1_plane{o}", align_bytes=64)
-            nc.vector.quantize_mx(codes[:].bitcast(FP8X4), plane[:], grouped[:])
+            if o == 0:
+                nc.scalar.copy(grouped[:], woven)
+            else:
+                nc.scalar.copy(grouped[:, 320:H, :], woven[:, 320:H, :])
+                nc.vector.tensor_copy(grouped[:, 0 : H // 2, :], woven[:, 0 : H // 2, :])
+                nc.vector.tensor_copy(grouped[:, H // 2 : 320, :], woven[:, H // 2 : 320, :])
+            for half in range(2):
+                cols = slice(half * H // 2, (half + 1) * H // 2)
+                nc.vector.quantize_mx(
+                    codes[:, cols].bitcast(FP8X4), plane[:, cols], grouped[:, cols, :].rearrange("p c j -> p (c j)")
+                )
             w1_codes.append(codes)
             w1_planes.append(plane)
 
-        w2_plane = keep.tile([P, N], U8, name="w2_plane", tag="grouped1", align_bytes=64)
+        w2_plane = keep.tile([P, N], U8, name="w2_plane", tag="grouped0", align_bytes=64)
         nc.vector.memset(w2_plane[:].bitcast(I32), 0)
         for q in range(4):
             nc.sync.dma_start(
@@ -111,16 +124,11 @@ def tile_picked_zbloom_relu_p_kernel(
 
         y = [[psum.tile([P, H], F32, name=f"y{d}_{b}", tag=f"bank{d}_{b}") for b in range(BLOCKS)] for d in range(D)]
         for o in range(PASSES):
-            for d in range(D):
-                picked = keep.tile([P, V], U32, name=f"picked{o}_{d}", align_bytes=64)
-                nc.vector.tensor_copy(
-                    picked[:],
-                    table_words[o][:].bitcast(U32).indirect(offsets[:, d * V // 16 : (d + 1) * V // 16]),
-                )
-                for b in range(BLOCKS):
+            for b in range(BLOCKS):
+                for d in range(D):
                     nc.tensor.matmul_mx(
                         y[d][b][:],
-                        lhsT=picked[:, b * P : (b + 1) * P].bitcast(FP8X4),
+                        lhsT=picked[D * o + d][:, b * P : (b + 1) * P].bitcast(FP8X4),
                         lhsT_scale=picked_planes[o][:, d * V + b * P : d * V + (b + 1) * P],
                         rhs=w1_codes[o][:].bitcast(FP8X4),
                         rhs_scale=w1_planes[o][:],
@@ -128,26 +136,36 @@ def tile_picked_zbloom_relu_p_kernel(
                         stop=(o == PASSES - 1),
                     )
 
-        firsts = []
+        def pairs_of(bank, u):
+            return bank[:].rearrange("p (m u e) -> p u m e", u=2, e=2)[:, u]
+
+        turned = []
         for b in range(BLOCKS):
-            first = keep.tile([P, H], F32, name=f"first{b}")
-            nc.scalar.activation(first[:], y[0][b][:], ACT.Copy, scale=gate_cols[:, b : b + 1])
-            firsts.append(first)
-        for b in range(BLOCKS):
-            summed = keep.tile([P, H], BF16, name=f"summed{b}", align_bytes=64)
-            nc.vector.scalar_tensor_tensor(
-                summed[:], y[1][b][:], gate_cols[:, BLOCKS + b : BLOCKS + b + 1], firsts[b][:], ALU.mult, ALU.add
-            )
-            turned = psum.tile([P, 2, P], F32, name=f"turned{b}", tag=f"bank0_{b}")
-            pairs = summed[:].bitcast(F32)
+            sums = []
             for u in range(2):
-                nc.tensor.transpose(turned[:, u, :], pairs[:, u * P : (u + 1) * P], identity[:])
+                first = keep.tile([P, P, 2], F32, name=f"first{b}_{u}")
+                nc.scalar.activation(first[:], pairs_of(y[0][b], u), ACT.Copy, scale=gate_cols[:, b : b + 1])
+                summed = keep.tile([P, P, 2], BF16, name=f"summed{b}_{u}", align_bytes=64)
+                nc.vector.scalar_tensor_tensor(
+                    summed[:], pairs_of(y[1][b], u), gate_cols[:, BLOCKS + b : BLOCKS + b + 1], first[:], ALU.mult, ALU.add
+                )
+                sums.append(summed)
+            bank = psum.tile([P, 2, P], F32, name=f"turned{b}", tag=f"bank0_{b}")
+            for u in range(2):
+                nc.tensor.transpose(bank[:, u, :], sums[u][:].rearrange("p m e -> p (m e)").bitcast(F32), identity[:])
+            turned.append(bank)
+
+        def relu(b):
             z = keep.tile([P, P * PACK], BF16, name=f"z{b}", align_bytes=64)
-            nc.scalar.activation(
-                z[:].rearrange("p (v u e) -> p v u e", u=2, e=2),
-                turned[:].rearrange("p u v -> p (u v)").bitcast(BF16).rearrange("p (u v e) -> p v u e", u=2, e=2),
-                ACT.Relu,
-            )
+            woven = z[:].rearrange("p (v u e) -> p v u e", u=2, e=2)
+            halves = turned[b][:].rearrange("p u v -> p (u v)").bitcast(BF16).rearrange("p (u v e) -> p v u e", u=2, e=2)
+            if b % 2 == 0:
+                nc.scalar.activation(woven, halves, ACT.Relu)
+            else:
+                nc.vector.tensor_scalar_max(woven, halves, 0.0)
+            return z
+
+        def second_layer(b, z):
             z_codes = keep.tile([P, P], U32, name=f"z_codes{b}", align_bytes=64)
             z_plane = keep.tile([P, P], U8, name=f"z_plane{b}", align_bytes=64)
             nc.vector.quantize_mx(z_codes[:].bitcast(FP8X4), z_plane[:], z[:])
@@ -162,5 +180,10 @@ def tile_picked_zbloom_relu_p_kernel(
                 stop=True,
             )
             result = keep.tile([N, P], F32, name=f"result{b}")
-            nc.vector.tensor_copy(result[:], acc[:])
-            nc.sync.dma_start(out[:, b * P : (b + 1) * P], result[:])
+            nc.scalar.copy(result[:], acc[:])
+            queue = nc.sync if b < BLOCKS - 1 else nc.scalar
+            queue.dma_start(out[:, b * P : (b + 1) * P], result[:])
+
+        zs = [relu(b) for b in range(BLOCKS)]
+        for b in range(BLOCKS):
+            second_layer(b, zs[b])

@@ -22,6 +22,7 @@ P = 128
 PACK = 4
 PASSES = K // (P * PACK)
 BLOCKS = V // P
+SPLIT = 3 * T // 4
 
 
 def tile_picked_zbloom_relu_p_kernel(
@@ -30,35 +31,32 @@ def tile_picked_zbloom_relu_p_kernel(
     nc = tc.nc
     with ExitStack() as ctx:
         keep = ctx.enter_context(tc.tile_pool(name="keep", bufs=1))
+        shared = ctx.enter_context(tc.tile_pool(name="shared", bufs=1))
         psum = ctx.enter_context(tc.psum_pool(name="psum", bufs=1))
 
-        table_scales = keep.tile([P, T], U8, name="table_scales", tag="scales_then_w1", align_bytes=64)
+        table_scales = shared.tile([P, T], U8, name="table_scales", align_bytes=64, offset=6144)
         nc.sync.dma_start(
             table_scales[96:P, :].bitcast(I32), x_scales.rearrange("o q n -> (o q) n").bitcast(I32)
         )
         nc.vector.memset(table_scales[0:96, :].bitcast(I32), 0)
 
-        def load_w1(o, tag):
-            raw = keep.tile([P, PACK, H], F32, name=f"w1_raw{o}", tag=tag, align_bytes=64)
+        offsets = keep.tile([P, S // 16], U16, name="offsets")
+        nc.sync.dma_start(offsets[:], offs)
+
+        def load_w1(o, raw):
             nc.sync.dma_start(raw[:], w1[512 * o : 512 * (o + 1), :].rearrange("(p j) c -> p j c", j=PACK))
             return raw
 
-        w1_raw = [load_w1(0, "w1")]
-        offsets = keep.tile([P, S // 16], U16, name="offsets")
-        nc.sync.dma_start(offsets[:], offs)
+        w1_raw = [load_w1(0, keep.tile([P, PACK, H], F32, name="w1_raw0", align_bytes=64))]
         gate_rows = keep.tile([P, P], F32, name="gate_rows")
         nc.sync.dma_start(
             gate_rows[P - D * BLOCKS : P, :], gate[:, 0, :].rearrange("d (b p) -> d b p", p=P)
         )
         nc.vector.memset(gate_rows[0:96, :], 0.0)
         nc.vector.memset(gate_rows[96 : P - D * BLOCKS, :], 0.0)
-        w2_codes = keep.tile([P, 2 * N], U8, name="w2_codes", align_bytes=64)
-        nc.sync.dma_start(w2_codes[:].bitcast(I32), w2_words[0].bitcast(I32))
-        table_words = []
-        for o in range(PASSES):
-            words = keep.tile([P, T], I32, name=f"table_words{o}", align_bytes=64)
-            nc.sync.dma_start(words[:], x_words[o].rearrange("p n t -> p (n t)").bitcast(I32))
-            table_words.append(words)
+        x_rows = [x_words[o].rearrange("p n t -> p (n t)").bitcast(I32) for o in range(PASSES)]
+        table_words = [keep.tile([P, T], I32, name="table_words0", align_bytes=64)]
+        nc.sync.dma_start(table_words[0][:], x_rows[0])
 
         identity = keep.tile([P, P], F32, name="identity")
         make_identity(nc, identity[:])
@@ -81,8 +79,13 @@ def tile_picked_zbloom_relu_p_kernel(
                 )
             return plane
 
+        table_words.append(shared.tile([P, T], I32, name="table_words1", align_bytes=64, offset=8448))
+        nc.sync.dma_start(table_words[1][:, 0:SPLIT], x_rows[1][:, 0:SPLIT])
         picked_planes = [place_scales(0)]
-        w1_raw.append(load_w1(1, "scales_then_w1"))
+        nc.sync.dma_start(table_words[1][:, SPLIT:T], x_rows[1][:, SPLIT:T])
+        w1_raw.append(load_w1(1, shared.tile([P, PACK, H], F32, name="w1_raw1", align_bytes=64, offset=0)))
+        w2_codes = shared.tile([P, 2 * N], U8, name="w2_codes", align_bytes=64, offset=8192)
+        nc.sync.dma_start(w2_codes[:].bitcast(I32), w2_words[0].bitcast(I32))
         picked_planes.append(place_scales(1))
 
         picked = []
@@ -98,15 +101,21 @@ def tile_picked_zbloom_relu_p_kernel(
         w1_codes, w1_planes = [], []
         for o in range(PASSES):
             grouped = keep.tile([P, H, PACK], BF16, name=f"w1_grouped{o}", tag=f"grouped{o}", align_bytes=64)
-            woven = w1_raw[o][:].rearrange("p j c -> p c j")
+
+            def weave(engine_copy, lo, hi):
+                engine_copy(
+                    grouped[:, lo:hi, :].rearrange("p (c i) j -> p c j i", i=4),
+                    w1_raw[o][:, :, lo:hi].rearrange("p j (c i) -> p c j i", i=4),
+                )
+
             codes = keep.tile([P, H], U32, name=f"w1_codes{o}", align_bytes=64)
             plane = keep.tile([P, H], U8, name=f"w1_plane{o}", align_bytes=64)
             if o == 0:
-                nc.scalar.copy(grouped[:], woven)
+                weave(nc.scalar.copy, 0, H)
             else:
-                nc.scalar.copy(grouped[:, 320:H, :], woven[:, 320:H, :])
-                nc.vector.tensor_copy(grouped[:, 0 : H // 2, :], woven[:, 0 : H // 2, :])
-                nc.vector.tensor_copy(grouped[:, H // 2 : 320, :], woven[:, H // 2 : 320, :])
+                weave(nc.scalar.copy, 320, H)
+                weave(nc.vector.tensor_copy, 0, H // 2)
+                weave(nc.vector.tensor_copy, H // 2, 320)
             for half in range(2):
                 cols = slice(half * H // 2, (half + 1) * H // 2)
                 nc.vector.quantize_mx(
@@ -123,33 +132,58 @@ def tile_picked_zbloom_relu_p_kernel(
             )
 
         y = [[psum.tile([P, H], F32, name=f"y{d}_{b}", tag=f"bank{d}_{b}") for b in range(BLOCKS)] for d in range(D)]
-        for o in range(PASSES):
-            for b in range(BLOCKS):
-                for d in range(D):
-                    nc.tensor.matmul_mx(
-                        y[d][b][:],
-                        lhsT=picked[D * o + d][:, b * P : (b + 1) * P].bitcast(FP8X4),
-                        lhsT_scale=picked_planes[o][:, d * V + b * P : d * V + (b + 1) * P],
-                        rhs=w1_codes[o][:].bitcast(FP8X4),
-                        rhs_scale=w1_planes[o][:],
-                        start=(o == 0),
-                        stop=(o == PASSES - 1),
-                    )
+
+        def first_layer(o, b, d, lo, hi):
+            nc.tensor.matmul_mx(
+                y[d][b][:, lo:hi],
+                lhsT=picked[D * o + d][:, b * P : (b + 1) * P].bitcast(FP8X4),
+                lhsT_scale=picked_planes[o][:, d * V + b * P : d * V + (b + 1) * P],
+                rhs=w1_codes[o][:, lo:hi].bitcast(FP8X4),
+                rhs_scale=w1_planes[o][:, lo:hi],
+                start=(o == 0),
+                stop=(o == PASSES - 1 and hi == H),
+            )
+
+        for b in range(BLOCKS):
+            for d in range(D):
+                first_layer(0, b, d, 0, H)
+        for lo in (0, H // 2):
+            for d in range(D):
+                first_layer(1, 0, d, lo, lo + H // 2)
+        for b in range(1, BLOCKS):
+            for d in range(D):
+                first_layer(1, b, d, 0, H)
 
         def pairs_of(bank, u):
             return bank[:].rearrange("p (m u e) -> p u m e", u=2, e=2)[:, u]
 
         turned = []
         for b in range(BLOCKS):
-            sums = []
-            for u in range(2):
-                first = keep.tile([P, P, 2], F32, name=f"first{b}_{u}")
-                nc.scalar.activation(first[:], pairs_of(y[0][b], u), ACT.Copy, scale=gate_cols[:, b : b + 1])
-                summed = keep.tile([P, P, 2], BF16, name=f"summed{b}_{u}", align_bytes=64)
+            gates = [gate_cols[:, d * BLOCKS + b : d * BLOCKS + b + 1] for d in range(D)]
+            firsts = [keep.tile([P, P, 2], F32, name=f"first{b}_{u}") for u in range(2)]
+            sums = [keep.tile([P, P, 2], BF16, name=f"summed{b}_{u}", align_bytes=64) for u in range(2)]
+
+            def scale_on_scalar(u, rows):
+                nc.scalar.activation(firsts[u][:, rows], pairs_of(y[0][b], u)[:, rows], ACT.Copy, scale=gates[0])
+
+            def add_hash(d, u, rows):
                 nc.vector.scalar_tensor_tensor(
-                    summed[:], pairs_of(y[1][b], u), gate_cols[:, BLOCKS + b : BLOCKS + b + 1], first[:], ALU.mult, ALU.add
+                    sums[u][:, rows], pairs_of(y[d][b], u)[:, rows], gates[d], firsts[u][:, rows], ALU.mult, ALU.add
                 )
-                sums.append(summed)
+
+            whole = slice(0, P)
+            if b == 0:
+                quarters = (slice(0, P // 2), slice(P // 2, P))
+                for rows in quarters:
+                    scale_on_scalar(0, rows)
+                nc.vector.tensor_scalar_mul(firsts[1][:], pairs_of(y[1][b], 1), gates[1])
+                for rows in quarters:
+                    add_hash(1, 0, rows)
+                add_hash(0, 1, whole)
+            else:
+                for u in range(2):
+                    scale_on_scalar(u, whole)
+                    add_hash(1, u, whole)
             bank = psum.tile([P, 2, P], F32, name=f"turned{b}", tag=f"bank0_{b}")
             for u in range(2):
                 nc.tensor.transpose(bank[:, u, :], sums[u][:].rearrange("p m e -> p (m e)").bitcast(F32), identity[:])

@@ -22,6 +22,7 @@ P = 128
 PACK = 4
 PASSES = K // (P * PACK)
 BLOCKS = V // P
+VECTOR_COLUMNS = 112
 SPLIT = 3 * T // 4
 
 
@@ -32,9 +33,11 @@ def tile_picked_zbloom_relu_p_kernel(
     with ExitStack() as ctx:
         keep = ctx.enter_context(tc.tile_pool(name="keep", bufs=1))
         shared = ctx.enter_context(tc.tile_pool(name="shared", bufs=1))
+        tail = ctx.enter_context(tc.tile_pool(name="tail", bufs=1))
+        later = ctx.enter_context(tc.tile_pool(name="later", bufs=1))
         psum = ctx.enter_context(tc.psum_pool(name="psum", bufs=1))
 
-        table_scales = shared.tile([P, T], U8, name="table_scales", align_bytes=64, offset=6144)
+        table_scales = shared.tile([P, T], U8, name="table_scales", align_bytes=64, offset=2048)
         nc.sync.dma_start(
             table_scales[96:P, :].bitcast(I32), x_scales.rearrange("o q n -> (o q) n").bitcast(I32)
         )
@@ -43,11 +46,11 @@ def tile_picked_zbloom_relu_p_kernel(
         offsets = keep.tile([P, S // 16], U16, name="offsets")
         nc.sync.dma_start(offsets[:], offs)
 
-        def load_w1(o, raw):
-            nc.sync.dma_start(raw[:], w1[512 * o : 512 * (o + 1), :].rearrange("(p j) c -> p j c", j=PACK))
+        def load_w1(o, raw, lo, hi):
+            nc.sync.dma_start(raw[:], w1[512 * o : 512 * (o + 1), lo:hi].rearrange("(p j) c -> p j c", j=PACK))
             return raw
 
-        w1_raw = [load_w1(0, keep.tile([P, PACK, H], F32, name="w1_raw0", align_bytes=64))]
+        w1_first = load_w1(0, later.tile([P, PACK, H], F32, name="w1_raw0", align_bytes=64, offset=0), 0, H)
         gate_rows = keep.tile([P, P], F32, name="gate_rows")
         nc.sync.dma_start(
             gate_rows[P - D * BLOCKS : P, :], gate[:, 0, :].rearrange("d (b p) -> d b p", p=P)
@@ -62,14 +65,22 @@ def tile_picked_zbloom_relu_p_kernel(
         make_identity(nc, identity[:])
         gate_turned = psum.tile([P, P], F32, name="gate_turned", tag="bank0_0")
         nc.tensor.transpose(gate_turned[:], gate_rows[:], identity[:])
-        gate_cols = keep.tile([P, D * BLOCKS], F32, name="gate_cols")
-        nc.scalar.activation(gate_cols[:], gate_turned[:, P - D * BLOCKS : P], ACT.Copy)
+        gate_cols = [
+            tail.tile([P, BLOCKS], F32, name="gate_cols0", align_bytes=64, offset=2048),
+            keep.tile([P, BLOCKS], F32, name="gate_cols1"),
+        ]
+        for d in range(D):
+            lo = P - (D - d) * BLOCKS
+            nc.scalar.activation(gate_cols[d][:], gate_turned[:, lo : lo + BLOCKS], ACT.Copy)
 
         gathered_scales = keep.tile([P, S], U8, name="gathered_scales", align_bytes=64)
         nc.vector.tensor_copy(gathered_scales[:], table_scales[:].indirect(offsets[:]))
 
         def place_scales(o):
-            plane = keep.tile([P, S], U8, name=f"picked_plane{o}", align_bytes=64)
+            if o == 0:
+                plane = keep.tile([P, S], U8, name="picked_plane0", align_bytes=64)
+            else:
+                plane = later.tile([P, S], U8, name="picked_plane1", align_bytes=64, offset=4608)
             nc.vector.memset(plane[:].bitcast(I32), 0)
             for q in range(4):
                 row = 96 + 16 * o + 4 * q
@@ -79,14 +90,11 @@ def tile_picked_zbloom_relu_p_kernel(
                 )
             return plane
 
-        table_words.append(shared.tile([P, T], I32, name="table_words1", align_bytes=64, offset=8448))
+        table_words.append(shared.tile([P, T], I32, name="table_words1", align_bytes=64, offset=4096))
         nc.sync.dma_start(table_words[1][:, 0:SPLIT], x_rows[1][:, 0:SPLIT])
         picked_planes = [place_scales(0)]
         nc.sync.dma_start(table_words[1][:, SPLIT:T], x_rows[1][:, SPLIT:T])
-        w1_raw.append(load_w1(1, shared.tile([P, PACK, H], F32, name="w1_raw1", align_bytes=64, offset=0)))
-        w2_codes = shared.tile([P, 2 * N], U8, name="w2_codes", align_bytes=64, offset=8192)
-        nc.sync.dma_start(w2_codes[:].bitcast(I32), w2_words[0].bitcast(I32))
-        picked_planes.append(place_scales(1))
+        w1_left = load_w1(1, shared.tile([P, PACK, H // 2], F32, name="w1_left", align_bytes=64, offset=0), 0, H // 2)
 
         picked = []
         for o in range(PASSES):
@@ -98,31 +106,36 @@ def tile_picked_zbloom_relu_p_kernel(
                 )
                 picked.append(words)
 
-        w1_codes, w1_planes = [], []
-        for o in range(PASSES):
-            grouped = keep.tile([P, H, PACK], BF16, name=f"w1_grouped{o}", tag=f"grouped{o}", align_bytes=64)
+        def weave(engine_copy, grouped, raw, lo, hi):
+            engine_copy(
+                grouped[:, lo:hi, :].rearrange("p (c i) j -> p c j i", i=4),
+                raw[:, :, lo:hi].rearrange("p j (c i) -> p c j i", i=4),
+            )
 
-            def weave(engine_copy, lo, hi):
-                engine_copy(
-                    grouped[:, lo:hi, :].rearrange("p (c i) j -> p c j i", i=4),
-                    w1_raw[o][:, :, lo:hi].rearrange("p j (c i) -> p c j i", i=4),
-                )
+        w1_codes = [keep.tile([P, H], U32, name=f"w1_codes{o}", align_bytes=64) for o in range(PASSES)]
+        w1_planes = [keep.tile([P, H], U8, name=f"w1_plane{o}", align_bytes=64) for o in range(PASSES)]
 
-            codes = keep.tile([P, H], U32, name=f"w1_codes{o}", align_bytes=64)
-            plane = keep.tile([P, H], U8, name=f"w1_plane{o}", align_bytes=64)
-            if o == 0:
-                weave(nc.scalar.copy, 0, H)
-            else:
-                weave(nc.scalar.copy, 320, H)
-                weave(nc.vector.tensor_copy, 0, H // 2)
-                weave(nc.vector.tensor_copy, H // 2, 320)
-            for half in range(2):
-                cols = slice(half * H // 2, (half + 1) * H // 2)
-                nc.vector.quantize_mx(
-                    codes[:, cols].bitcast(FP8X4), plane[:, cols], grouped[:, cols, :].rearrange("p c j -> p (c j)")
-                )
-            w1_codes.append(codes)
-            w1_planes.append(plane)
+        def quantise(o, lo, hi, grouped):
+            nc.vector.quantize_mx(
+                w1_codes[o][:, lo:hi].bitcast(FP8X4), w1_planes[o][:, lo:hi], grouped.rearrange("p c j -> p (c j)")
+            )
+
+        grouped = keep.tile([P, H, PACK], BF16, name="w1_grouped0", tag="grouped0", align_bytes=64)
+        weave(nc.scalar.copy, grouped, w1_first, 0, H)
+        quantise(0, 0, H, grouped[:])
+
+        w1_right = load_w1(1, later.tile([P, PACK, H // 2], F32, name="w1_right", align_bytes=64, offset=0), H // 2, H)
+        w2_codes = later.tile([P, 2 * N], U8, name="w2_codes", align_bytes=64, offset=4096)
+        nc.sync.dma_start(w2_codes[:].bitcast(I32), w2_words[0].bitcast(I32))
+        picked_planes.append(place_scales(1))
+
+        left = keep.tile([P, H // 2, PACK], BF16, name="w1_grouped_left", align_bytes=64)
+        right = keep.tile([P, H // 2, PACK], BF16, name="w1_grouped_right", align_bytes=64)
+        weave(nc.scalar.copy, left, w1_left, 0, H // 2)
+        weave(nc.scalar.copy, right, w1_right, VECTOR_COLUMNS, H // 2)
+        quantise(1, 0, H // 2, left[:])
+        weave(nc.vector.tensor_copy, right, w1_right, 0, VECTOR_COLUMNS)
+        quantise(1, H // 2, H, right[:])
 
         w2_plane = keep.tile([P, N], U8, name="w2_plane", tag="grouped0", align_bytes=64)
         nc.vector.memset(w2_plane[:].bitcast(I32), 0)
@@ -159,8 +172,12 @@ def tile_picked_zbloom_relu_p_kernel(
 
         turned = []
         for b in range(BLOCKS):
-            gates = [gate_cols[:, d * BLOCKS + b : d * BLOCKS + b + 1] for d in range(D)]
-            firsts = [keep.tile([P, P, 2], F32, name=f"first{b}_{u}") for u in range(2)]
+            gates = [gate_cols[d][:, b : b + 1] for d in range(D)]
+            firsts = [keep.tile([P, P, 2], F32, name=f"first{b}_0")]
+            if b == BLOCKS - 1:
+                firsts.append(tail.tile([P, P, 2], F32, name="first_last", align_bytes=64, offset=512))
+            else:
+                firsts.append(keep.tile([P, P, 2], F32, name=f"first{b}_1"))
             sums = [keep.tile([P, P, 2], BF16, name=f"summed{b}_{u}", align_bytes=64) for u in range(2)]
 
             def scale_on_scalar(u, rows):
@@ -190,7 +207,10 @@ def tile_picked_zbloom_relu_p_kernel(
             turned.append(bank)
 
         def relu(b):
-            z = keep.tile([P, P * PACK], BF16, name=f"z{b}", align_bytes=64)
+            if b < 2:
+                z = tail.tile([P, P * PACK], BF16, name=f"z{b}", align_bytes=64, offset=(2048, 0)[b])
+            else:
+                z = keep.tile([P, P * PACK], BF16, name=f"z{b}", align_bytes=64)
             woven = z[:].rearrange("p (v u e) -> p v u e", u=2, e=2)
             halves = turned[b][:].rearrange("p u v -> p (u v)").bitcast(BF16).rearrange("p (u v e) -> p v u e", u=2, e=2)
             if b % 2 == 0:
@@ -200,7 +220,10 @@ def tile_picked_zbloom_relu_p_kernel(
             return z
 
         def second_layer(b, z):
-            z_codes = keep.tile([P, P], U32, name=f"z_codes{b}", align_bytes=64)
+            if b == 0:
+                z_codes = tail.tile([P, P], U32, name="z_codes0", align_bytes=64, offset=1024)
+            else:
+                z_codes = keep.tile([P, P], U32, name=f"z_codes{b}", align_bytes=64)
             z_plane = keep.tile([P, P], U8, name=f"z_plane{b}", align_bytes=64)
             nc.vector.quantize_mx(z_codes[:].bitcast(FP8X4), z_plane[:], z[:])
             acc = psum.tile([N, P], F32, name=f"acc{b}", tag=f"bank1_{b}")

@@ -22,8 +22,8 @@ P = 128
 PACK = 4
 PASSES = K // (P * PACK)
 BLOCKS = V // P
-VECTOR_COLUMNS = 112
-SPLIT = 3 * T // 4
+VECTOR_COLUMNS = 128
+SPLIT = 5 * T // 8
 
 
 def tile_picked_zbloom_relu_p_kernel(
@@ -33,7 +33,6 @@ def tile_picked_zbloom_relu_p_kernel(
     with ExitStack() as ctx:
         keep = ctx.enter_context(tc.tile_pool(name="keep", bufs=1))
         shared = ctx.enter_context(tc.tile_pool(name="shared", bufs=1))
-        tail = ctx.enter_context(tc.tile_pool(name="tail", bufs=1))
         later = ctx.enter_context(tc.tile_pool(name="later", bufs=1))
         psum = ctx.enter_context(tc.psum_pool(name="psum", bufs=1))
 
@@ -65,13 +64,8 @@ def tile_picked_zbloom_relu_p_kernel(
         make_identity(nc, identity[:])
         gate_turned = psum.tile([P, P], F32, name="gate_turned", tag="bank0_0")
         nc.tensor.transpose(gate_turned[:], gate_rows[:], identity[:])
-        gate_cols = [
-            tail.tile([P, BLOCKS], F32, name="gate_cols0", align_bytes=64, offset=2048),
-            keep.tile([P, BLOCKS], F32, name="gate_cols1"),
-        ]
-        for d in range(D):
-            lo = P - (D - d) * BLOCKS
-            nc.scalar.activation(gate_cols[d][:], gate_turned[:, lo : lo + BLOCKS], ACT.Copy)
+        gate_cols = keep.tile([P, D * BLOCKS], F32, name="gate_cols")
+        nc.scalar.activation(gate_cols[:], gate_turned[:, P - D * BLOCKS : P], ACT.Copy)
 
         gathered_scales = keep.tile([P, S], U8, name="gathered_scales", align_bytes=64)
         nc.vector.tensor_copy(gathered_scales[:], table_scales[:].indirect(offsets[:]))
@@ -125,8 +119,6 @@ def tile_picked_zbloom_relu_p_kernel(
         quantise(0, 0, H, grouped[:])
 
         w1_right = load_w1(1, later.tile([P, PACK, H // 2], F32, name="w1_right", align_bytes=64, offset=0), H // 2, H)
-        w2_codes = later.tile([P, 2 * N], U8, name="w2_codes", align_bytes=64, offset=4096)
-        nc.sync.dma_start(w2_codes[:].bitcast(I32), w2_words[0].bitcast(I32))
         picked_planes.append(place_scales(1))
 
         left = keep.tile([P, H // 2, PACK], BF16, name="w1_grouped_left", align_bytes=64)
@@ -137,7 +129,9 @@ def tile_picked_zbloom_relu_p_kernel(
         weave(nc.vector.tensor_copy, right, w1_right, 0, VECTOR_COLUMNS)
         quantise(1, H // 2, H, right[:])
 
-        w2_plane = keep.tile([P, N], U8, name="w2_plane", tag="grouped0", align_bytes=64)
+        w2_codes = keep.tile([P, 2 * N], U8, name="w2_codes", tag="grouped0", align_bytes=64)
+        nc.sync.dma_start(w2_codes[:].bitcast(I32), w2_words[0].bitcast(I32))
+        w2_plane = later.tile([P, N], U8, name="w2_plane", align_bytes=64, offset=4096)
         nc.vector.memset(w2_plane[:].bitcast(I32), 0)
         for q in range(4):
             nc.sync.dma_start(
@@ -161,23 +155,20 @@ def tile_picked_zbloom_relu_p_kernel(
             for d in range(D):
                 first_layer(0, b, d, 0, H)
         for lo in (0, H // 2):
-            for d in range(D):
-                first_layer(1, 0, d, lo, lo + H // 2)
+            for b, d in ((0, 0), (0, 1), (1, 0)):
+                first_layer(1, b, d, lo, lo + H // 2)
         for b in range(1, BLOCKS):
-            for d in range(D):
-                first_layer(1, b, d, 0, H)
+            if b + 1 < BLOCKS:
+                first_layer(1, b + 1, 0, 0, H)
+            first_layer(1, b, 1, 0, H)
 
         def pairs_of(bank, u):
             return bank[:].rearrange("p (m u e) -> p u m e", u=2, e=2)[:, u]
 
         turned = []
         for b in range(BLOCKS):
-            gates = [gate_cols[d][:, b : b + 1] for d in range(D)]
-            firsts = [keep.tile([P, P, 2], F32, name=f"first{b}_0")]
-            if b == BLOCKS - 1:
-                firsts.append(tail.tile([P, P, 2], F32, name="first_last", align_bytes=64, offset=512))
-            else:
-                firsts.append(keep.tile([P, P, 2], F32, name=f"first{b}_1"))
+            gates = [gate_cols[:, d * BLOCKS + b : d * BLOCKS + b + 1] for d in range(D)]
+            firsts = [keep.tile([P, P, 2], F32, name=f"first{b}_{u}") for u in range(2)]
             sums = [keep.tile([P, P, 2], BF16, name=f"summed{b}_{u}", align_bytes=64) for u in range(2)]
 
             def scale_on_scalar(u, rows):
@@ -207,10 +198,7 @@ def tile_picked_zbloom_relu_p_kernel(
             turned.append(bank)
 
         def relu(b):
-            if b < 2:
-                z = tail.tile([P, P * PACK], BF16, name=f"z{b}", align_bytes=64, offset=(2048, 0)[b])
-            else:
-                z = keep.tile([P, P * PACK], BF16, name=f"z{b}", align_bytes=64)
+            z = keep.tile([P, P * PACK], BF16, name=f"z{b}", align_bytes=64)
             woven = z[:].rearrange("p (v u e) -> p v u e", u=2, e=2)
             halves = turned[b][:].rearrange("p u v -> p (u v)").bitcast(BF16).rearrange("p (u v e) -> p v u e", u=2, e=2)
             if b % 2 == 0:
@@ -220,10 +208,7 @@ def tile_picked_zbloom_relu_p_kernel(
             return z
 
         def second_layer(b, z):
-            if b == 0:
-                z_codes = tail.tile([P, P], U32, name="z_codes0", align_bytes=64, offset=1024)
-            else:
-                z_codes = keep.tile([P, P], U32, name=f"z_codes{b}", align_bytes=64)
+            z_codes = keep.tile([P, P], U32, name=f"z_codes{b}", align_bytes=64)
             z_plane = keep.tile([P, P], U8, name=f"z_plane{b}", align_bytes=64)
             nc.vector.quantize_mx(z_codes[:].bitcast(FP8X4), z_plane[:], z[:])
             acc = psum.tile([N, P], F32, name=f"acc{b}", tag=f"bank1_{b}")

@@ -22,8 +22,12 @@ P = 128
 PACK = 4
 PASSES = K // (P * PACK)
 BLOCKS = V // P
-VECTOR_COLUMNS = 128
-SPLIT = 5 * T // 8
+HALF = H // 2
+QUADRANTS = 4
+STAGE = P - 32
+LINE = 4
+VECTOR_COLUMNS = HALF // 2
+EARLY_COLUMNS = 3 * T // 4
 
 
 def tile_picked_zbloom_relu_p_kernel(
@@ -32,30 +36,32 @@ def tile_picked_zbloom_relu_p_kernel(
     nc = tc.nc
     with ExitStack() as ctx:
         keep = ctx.enter_context(tc.tile_pool(name="keep", bufs=1))
-        shared = ctx.enter_context(tc.tile_pool(name="shared", bufs=1))
-        later = ctx.enter_context(tc.tile_pool(name="later", bufs=1))
+        after_scales = ctx.enter_context(tc.tile_pool(name="after_scales", bufs=1))
+        after_cast = ctx.enter_context(tc.tile_pool(name="after_cast", bufs=1))
         psum = ctx.enter_context(tc.psum_pool(name="psum", bufs=1))
 
-        table_scales = shared.tile([P, T], U8, name="table_scales", align_bytes=64, offset=2048)
+        table_scales = after_scales.tile([P, T], U8, name="table_scales", align_bytes=64, offset=2048)
         nc.sync.dma_start(
-            table_scales[96:P, :].bitcast(I32), x_scales.rearrange("o q n -> (o q) n").bitcast(I32)
+            table_scales[STAGE:P, :].bitcast(I32), x_scales.rearrange("o q n -> (o q) n").bitcast(I32)
         )
-        nc.vector.memset(table_scales[0:96, :].bitcast(I32), 0)
+        nc.vector.memset(table_scales[0:STAGE, :].bitcast(I32), 0)
 
         offsets = keep.tile([P, S // 16], U16, name="offsets")
         nc.sync.dma_start(offsets[:], offs)
 
         def load_w1(o, raw, lo, hi):
-            nc.sync.dma_start(raw[:], w1[512 * o : 512 * (o + 1), lo:hi].rearrange("(p j) c -> p j c", j=PACK))
-            return raw
+            rows = w1[P * PACK * o : P * PACK * (o + 1), lo:hi]
+            nc.sync.dma_start(raw[:], rows.rearrange("(p j) c -> p j c", j=PACK))
 
-        w1_first = load_w1(0, later.tile([P, PACK, H], F32, name="w1_raw0", align_bytes=64, offset=0), 0, H)
+        w1_first = after_cast.tile([P, PACK, H], F32, name="w1_first", align_bytes=64, offset=0)
+        load_w1(0, w1_first, 0, H)
+
+        gate_start = P - D * BLOCKS
         gate_rows = keep.tile([P, P], F32, name="gate_rows")
-        nc.sync.dma_start(
-            gate_rows[P - D * BLOCKS : P, :], gate[:, 0, :].rearrange("d (b p) -> d b p", p=P)
-        )
-        nc.vector.memset(gate_rows[0:96, :], 0.0)
-        nc.vector.memset(gate_rows[96 : P - D * BLOCKS, :], 0.0)
+        nc.sync.dma_start(gate_rows[gate_start:P, :], gate[:, 0, :].rearrange("d (b p) -> d b p", p=P))
+        nc.vector.memset(gate_rows[0:STAGE, :], 0.0)
+        nc.vector.memset(gate_rows[STAGE:gate_start, :], 0.0)
+
         x_rows = [x_words[o].rearrange("p n t -> p (n t)").bitcast(I32) for o in range(PASSES)]
         table_words = [keep.tile([P, T], I32, name="table_words0", align_bytes=64)]
         nc.sync.dma_start(table_words[0][:], x_rows[0])
@@ -65,35 +71,32 @@ def tile_picked_zbloom_relu_p_kernel(
         gate_turned = psum.tile([P, P], F32, name="gate_turned", tag="bank0_0")
         nc.tensor.transpose(gate_turned[:], gate_rows[:], identity[:])
         gate_cols = keep.tile([P, D * BLOCKS], F32, name="gate_cols")
-        nc.scalar.activation(gate_cols[:], gate_turned[:, P - D * BLOCKS : P], ACT.Copy)
+        nc.scalar.activation(gate_cols[:], gate_turned[:, gate_start:P], ACT.Copy)
 
         gathered_scales = keep.tile([P, S], U8, name="gathered_scales", align_bytes=64)
         nc.vector.tensor_copy(gathered_scales[:], table_scales[:].indirect(offsets[:]))
 
-        def place_scales(o):
-            if o == 0:
-                plane = keep.tile([P, S], U8, name="picked_plane0", align_bytes=64)
-            else:
-                plane = later.tile([P, S], U8, name="picked_plane1", align_bytes=64, offset=4608)
+        def place_scales(o, plane):
             nc.vector.memset(plane[:].bitcast(I32), 0)
-            for q in range(4):
-                row = 96 + 16 * o + 4 * q
+            for q in range(QUADRANTS):
+                row = STAGE + 16 * o + 4 * q
                 nc.sync.dma_start(
                     plane[32 * q : 32 * q + 4, :].bitcast(I32),
                     gathered_scales[row : row + 4, :].bitcast(I32),
                 )
-            return plane
 
-        table_words.append(shared.tile([P, T], I32, name="table_words1", align_bytes=64, offset=4096))
-        nc.sync.dma_start(table_words[1][:, 0:SPLIT], x_rows[1][:, 0:SPLIT])
-        picked_planes = [place_scales(0)]
-        nc.sync.dma_start(table_words[1][:, SPLIT:T], x_rows[1][:, SPLIT:T])
-        w1_left = load_w1(1, shared.tile([P, PACK, H // 2], F32, name="w1_left", align_bytes=64, offset=0), 0, H // 2)
+        table_words.append(after_scales.tile([P, T], I32, name="table_words1", align_bytes=64, offset=4096))
+        nc.sync.dma_start(table_words[1][:, 0:EARLY_COLUMNS], x_rows[1][:, 0:EARLY_COLUMNS])
+        picked_planes = [keep.tile([P, S], U8, name="picked_plane0", align_bytes=64)]
+        place_scales(0, picked_planes[0])
+        nc.sync.dma_start(table_words[1][:, EARLY_COLUMNS:T], x_rows[1][:, EARLY_COLUMNS:T])
+        w1_left = after_scales.tile([P, PACK, HALF], F32, name="w1_left", align_bytes=64, offset=0)
+        load_w1(1, w1_left, 0, HALF)
 
         picked = []
         for o in range(PASSES):
             for d in range(D):
-                words = keep.tile([P, V], U32, name=f"picked{o}_{d}", tag=f"picked{o}_{d}", align_bytes=64)
+                words = keep.tile([P, V], U32, name=f"picked{o}_{d}", align_bytes=64)
                 nc.vector.tensor_copy(
                     words[:],
                     table_words[o][:].bitcast(U32).indirect(offsets[:, d * V // 16 : (d + 1) * V // 16]),
@@ -102,38 +105,40 @@ def tile_picked_zbloom_relu_p_kernel(
 
         def weave(engine_copy, grouped, raw, lo, hi):
             engine_copy(
-                grouped[:, lo:hi, :].rearrange("p (c i) j -> p c j i", i=4),
-                raw[:, :, lo:hi].rearrange("p j (c i) -> p c j i", i=4),
+                grouped[:, lo:hi, :].rearrange("p (c i) j -> p c j i", i=LINE),
+                raw[:, :, lo:hi].rearrange("p j (c i) -> p c j i", i=LINE),
             )
 
         w1_codes = [keep.tile([P, H], U32, name=f"w1_codes{o}", align_bytes=64) for o in range(PASSES)]
         w1_planes = [keep.tile([P, H], U8, name=f"w1_plane{o}", align_bytes=64) for o in range(PASSES)]
 
-        def quantise(o, lo, hi, grouped):
+        def quantise_w1(o, lo, hi, grouped):
             nc.vector.quantize_mx(
-                w1_codes[o][:, lo:hi].bitcast(FP8X4), w1_planes[o][:, lo:hi], grouped.rearrange("p c j -> p (c j)")
+                w1_codes[o][:, lo:hi].bitcast(FP8X4), w1_planes[o][:, lo:hi], grouped[:].rearrange("p c j -> p (c j)")
             )
 
-        grouped = keep.tile([P, H, PACK], BF16, name="w1_grouped0", tag="grouped0", align_bytes=64)
-        weave(nc.scalar.copy, grouped, w1_first, 0, H)
-        quantise(0, 0, H, grouped[:])
+        grouped_first = keep.tile([P, H, PACK], BF16, name="grouped_first", tag="grouped_then_w2", align_bytes=64)
+        weave(nc.scalar.copy, grouped_first, w1_first, 0, H)
+        quantise_w1(0, 0, H, grouped_first)
 
-        w1_right = load_w1(1, later.tile([P, PACK, H // 2], F32, name="w1_right", align_bytes=64, offset=0), H // 2, H)
-        picked_planes.append(place_scales(1))
+        w1_right = after_cast.tile([P, PACK, HALF], F32, name="w1_right", align_bytes=64, offset=0)
+        load_w1(1, w1_right, HALF, H)
+        picked_planes.append(after_cast.tile([P, S], U8, name="picked_plane1", align_bytes=64, offset=4608))
+        place_scales(1, picked_planes[1])
 
-        left = keep.tile([P, H // 2, PACK], BF16, name="w1_grouped_left", align_bytes=64)
-        right = keep.tile([P, H // 2, PACK], BF16, name="w1_grouped_right", align_bytes=64)
-        weave(nc.scalar.copy, left, w1_left, 0, H // 2)
-        weave(nc.scalar.copy, right, w1_right, VECTOR_COLUMNS, H // 2)
-        quantise(1, 0, H // 2, left[:])
-        weave(nc.vector.tensor_copy, right, w1_right, 0, VECTOR_COLUMNS)
-        quantise(1, H // 2, H, right[:])
+        grouped_left = keep.tile([P, HALF, PACK], BF16, name="grouped_left", align_bytes=64)
+        grouped_right = keep.tile([P, HALF, PACK], BF16, name="grouped_right", align_bytes=64)
+        weave(nc.scalar.copy, grouped_left, w1_left, 0, HALF)
+        weave(nc.scalar.copy, grouped_right, w1_right, VECTOR_COLUMNS, HALF)
+        quantise_w1(1, 0, HALF, grouped_left)
+        weave(nc.vector.tensor_copy, grouped_right, w1_right, 0, VECTOR_COLUMNS)
+        quantise_w1(1, HALF, H, grouped_right)
 
-        w2_codes = keep.tile([P, 2 * N], U8, name="w2_codes", tag="grouped0", align_bytes=64)
+        w2_codes = keep.tile([P, 2 * N], U8, name="w2_codes", tag="grouped_then_w2", align_bytes=64)
         nc.sync.dma_start(w2_codes[:].bitcast(I32), w2_words[0].bitcast(I32))
-        w2_plane = later.tile([P, N], U8, name="w2_plane", align_bytes=64, offset=4096)
+        w2_plane = after_cast.tile([P, N], U8, name="w2_plane", align_bytes=64, offset=4096)
         nc.vector.memset(w2_plane[:].bitcast(I32), 0)
-        for q in range(4):
+        for q in range(QUADRANTS):
             nc.sync.dma_start(
                 w2_plane[32 * q : 32 * q + 4, :].bitcast(I32), w2_scales[0, 4 * q : 4 * q + 4, :].bitcast(I32)
             )
@@ -154,9 +159,9 @@ def tile_picked_zbloom_relu_p_kernel(
         for b in range(BLOCKS):
             for d in range(D):
                 first_layer(0, b, d, 0, H)
-        for lo in (0, H // 2):
+        for lo in (0, HALF):
             for b, d in ((0, 0), (0, 1), (1, 0)):
-                first_layer(1, b, d, lo, lo + H // 2)
+                first_layer(1, b, d, lo, lo + HALF)
         for b in range(1, BLOCKS):
             if b + 1 < BLOCKS:
                 first_layer(1, b + 1, 0, 0, H)
@@ -168,30 +173,30 @@ def tile_picked_zbloom_relu_p_kernel(
         turned = []
         for b in range(BLOCKS):
             gates = [gate_cols[:, d * BLOCKS + b : d * BLOCKS + b + 1] for d in range(D)]
-            firsts = [keep.tile([P, P, 2], F32, name=f"first{b}_{u}") for u in range(2)]
-            sums = [keep.tile([P, P, 2], BF16, name=f"summed{b}_{u}", align_bytes=64) for u in range(2)]
+            scaled = [keep.tile([P, P, 2], F32, name=f"scaled{b}_{u}") for u in range(2)]
+            sums = [keep.tile([P, P, 2], BF16, name=f"sums{b}_{u}", align_bytes=64) for u in range(2)]
 
-            def scale_on_scalar(u, rows):
-                nc.scalar.activation(firsts[u][:, rows], pairs_of(y[0][b], u)[:, rows], ACT.Copy, scale=gates[0])
+            def scale_hash0(u, pairs):
+                nc.scalar.activation(scaled[u][:, pairs], pairs_of(y[0][b], u)[:, pairs], ACT.Copy, scale=gates[0])
 
-            def add_hash(d, u, rows):
+            def add_hash(d, u, pairs):
                 nc.vector.scalar_tensor_tensor(
-                    sums[u][:, rows], pairs_of(y[d][b], u)[:, rows], gates[d], firsts[u][:, rows], ALU.mult, ALU.add
+                    sums[u][:, pairs], pairs_of(y[d][b], u)[:, pairs], gates[d], scaled[u][:, pairs], ALU.mult, ALU.add
                 )
 
-            whole = slice(0, P)
+            all_pairs = slice(0, P)
             if b == 0:
-                quarters = (slice(0, P // 2), slice(P // 2, P))
-                for rows in quarters:
-                    scale_on_scalar(0, rows)
-                nc.vector.tensor_scalar_mul(firsts[1][:], pairs_of(y[1][b], 1), gates[1])
-                for rows in quarters:
-                    add_hash(1, 0, rows)
-                add_hash(0, 1, whole)
+                pieces = (slice(0, P // 2), slice(P // 2, P))
+                for pairs in pieces:
+                    scale_hash0(0, pairs)
+                nc.vector.tensor_scalar_mul(scaled[1][:], pairs_of(y[1][b], 1), gates[1])
+                for pairs in pieces:
+                    add_hash(1, 0, pairs)
+                add_hash(0, 1, all_pairs)
             else:
                 for u in range(2):
-                    scale_on_scalar(u, whole)
-                    add_hash(1, u, whole)
+                    scale_hash0(u, all_pairs)
+                    add_hash(1, u, all_pairs)
             bank = psum.tile([P, 2, P], F32, name=f"turned{b}", tag=f"bank0_{b}")
             for u in range(2):
                 nc.tensor.transpose(bank[:, u, :], sums[u][:].rearrange("p m e -> p (m e)").bitcast(F32), identity[:])

@@ -25,6 +25,8 @@ BLOCKS = V // P
 HALF = H // 2
 QUADRANTS = 4
 STAGE = P - 32
+GATE_STEP = D * P * BLOCKS // (D * BLOCKS) + 1
+SHIFT = (12, 0)
 LINE = 4
 VECTOR_COLUMNS = HALF // 2
 EARLY_COLUMNS = 3 * T // 4
@@ -54,17 +56,17 @@ def tile_picked_zbloom_relu_p_kernel(
             nc.sync.dma_start(raw[:], rows.rearrange("(p j) c -> p j c", j=PACK))
 
         w1_first = after_cast.tile([P, PACK, H], F32, name="w1_first", align_bytes=64, offset=0)
-        load_w1(0, w1_first, 0, H)
 
         gate_start = P - D * BLOCKS
         gate_rows = keep.tile([P, P], F32, name="gate_rows")
-        nc.sync.dma_start(gate_rows[gate_start:P, :], gate[:, 0, :].rearrange("d (b p) -> d b p", p=P))
+        nc.sync.dma_start(gate_rows[gate_start:P, :], gate.rearrange("d r (b p) -> (d r b) p", p=P)[0 : D * P * BLOCKS : GATE_STEP])
         nc.vector.memset(gate_rows[0:STAGE, :], 0.0)
         nc.vector.memset(gate_rows[STAGE:gate_start, :], 0.0)
 
         x_rows = [x_words[o].rearrange("p n t -> p (n t)").bitcast(I32) for o in range(PASSES)]
         table_words = [keep.tile([P, T], I32, name="table_words0", align_bytes=64)]
         nc.sync.dma_start(table_words[0][:], x_rows[0])
+        load_w1(0, w1_first, 0, H)
 
         identity = keep.tile([P, P], F32, name="identity")
         make_identity(nc, identity[:])
@@ -77,19 +79,21 @@ def tile_picked_zbloom_relu_p_kernel(
         nc.vector.tensor_copy(gathered_scales[:], table_scales[:].indirect(offsets[:]))
 
         def place_scales(o, plane):
-            nc.vector.memset(plane[:].bitcast(I32), 0)
-            for q in range(QUADRANTS):
+            if o == 0:
+                nc.vector.tensor_copy(plane[:].bitcast(I32), gathered_scales[:].bitcast(I32))
+            else:
+                nc.vector.memset(plane[:].bitcast(I32), 0)
+            for q in range(QUADRANTS - 1 if o == 0 else QUADRANTS):
                 row = STAGE + 16 * o + 4 * q
                 nc.sync.dma_start(
-                    plane[32 * q : 32 * q + 4, :].bitcast(I32),
+                    plane[32 * q + SHIFT[o] : 32 * q + SHIFT[o] + 4, :].bitcast(I32),
                     gathered_scales[row : row + 4, :].bitcast(I32),
                 )
 
         table_words.append(after_scales.tile([P, T], I32, name="table_words1", align_bytes=64, offset=4096))
-        nc.sync.dma_start(table_words[1][:, 0:EARLY_COLUMNS], x_rows[1][:, 0:EARLY_COLUMNS])
         picked_planes = [keep.tile([P, S], U8, name="picked_plane0", align_bytes=64)]
         place_scales(0, picked_planes[0])
-        nc.sync.dma_start(table_words[1][:, EARLY_COLUMNS:T], x_rows[1][:, EARLY_COLUMNS:T])
+        nc.sync.dma_start(table_words[1][:], x_rows[1])
         w1_left = after_scales.tile([P, PACK, HALF], F32, name="w1_left", align_bytes=64, offset=0)
         load_w1(1, w1_left, 0, HALF)
 
@@ -149,7 +153,7 @@ def tile_picked_zbloom_relu_p_kernel(
             nc.tensor.matmul_mx(
                 y[d][b][:, lo:hi],
                 lhsT=picked[D * o + d][:, b * P : (b + 1) * P].bitcast(FP8X4),
-                lhsT_scale=picked_planes[o][:, d * V + b * P : d * V + (b + 1) * P],
+                lhsT_scale=picked_planes[o][SHIFT[o] : P, d * V + b * P : d * V + (b + 1) * P],
                 rhs=w1_codes[o][:, lo:hi].bitcast(FP8X4),
                 rhs_scale=w1_planes[o][:, lo:hi],
                 start=(o == 0),

@@ -59,7 +59,7 @@ def tile_picked_zbloom_relu_p_kernel(
 
         gate_start = P - D * BLOCKS
         gate_rows = keep.tile([P, P], F32, name="gate_rows")
-        nc.sync.dma_start(gate_rows[gate_start:P, :], gate.rearrange("d r (b p) -> (d r b) p", p=P)[0 : D * P * BLOCKS : GATE_STEP])
+        nc.scalar.dma_start(gate_rows[gate_start:P, :], gate.rearrange("d r (b p) -> (d r b) p", p=P)[0 : D * P * BLOCKS : GATE_STEP])
         nc.vector.memset(gate_rows[0:STAGE, :], 0.0)
         nc.vector.memset(gate_rows[STAGE:gate_start, :], 0.0)
 
@@ -122,7 +122,7 @@ def tile_picked_zbloom_relu_p_kernel(
             )
 
         grouped_first = keep.tile([P, H, PACK], BF16, name="grouped_first", tag="grouped_then_w2", align_bytes=64)
-        weave(nc.scalar.copy, grouped_first, w1_first, 0, H)
+        nc.scalar.copy(grouped_first[:], w1_first[:].rearrange("p j c -> p c j"))
         quantise_w1(0, 0, H, grouped_first)
 
         w1_right = after_cast.tile([P, PACK, HALF], F32, name="w1_right", align_bytes=64, offset=0)

@@ -25,11 +25,10 @@ BLOCKS = V // P
 HALF = H // 2
 QUADRANTS = 4
 STAGE = P - 32
-GATE_STEP = D * P * BLOCKS // (D * BLOCKS) + 1
+GATE_STEP = 32 * BLOCKS + 1
 SHIFT = (12, 0)
 LINE = 4
 VECTOR_COLUMNS = HALF // 2
-EARLY_COLUMNS = 3 * T // 4
 
 
 def tile_picked_zbloom_relu_p_kernel(
@@ -59,7 +58,8 @@ def tile_picked_zbloom_relu_p_kernel(
 
         gate_start = P - D * BLOCKS
         gate_rows = keep.tile([P, P], F32, name="gate_rows")
-        nc.scalar.dma_start(gate_rows[gate_start:P, :], gate.rearrange("d r (b p) -> (d r b) p", p=P)[0 : D * P * BLOCKS : GATE_STEP])
+        gate_pieces = gate.rearrange("d r (b p) -> (d r b) p", p=P)
+        nc.scalar.dma_start(gate_rows[gate_start:P, :], gate_pieces[0 : D * P * BLOCKS : GATE_STEP])
         nc.vector.memset(gate_rows[0:STAGE, :], 0.0)
         nc.vector.memset(gate_rows[STAGE:gate_start, :], 0.0)
 
@@ -81,9 +81,11 @@ def tile_picked_zbloom_relu_p_kernel(
         def place_scales(o, plane):
             if o == 0:
                 nc.vector.tensor_copy(plane[:].bitcast(I32), gathered_scales[:].bitcast(I32))
+                moved = QUADRANTS - 1
             else:
                 nc.vector.memset(plane[:].bitcast(I32), 0)
-            for q in range(QUADRANTS - 1 if o == 0 else QUADRANTS):
+                moved = QUADRANTS
+            for q in range(moved):
                 row = STAGE + 16 * o + 4 * q
                 nc.sync.dma_start(
                     plane[32 * q + SHIFT[o] : 32 * q + SHIFT[o] + 4, :].bitcast(I32),
@@ -231,9 +233,11 @@ def tile_picked_zbloom_relu_p_kernel(
                 stop=True,
             )
             result = keep.tile([N, P], F32, name=f"result{b}")
-            nc.scalar.copy(result[:], acc[:])
-            queue = nc.sync if b < BLOCKS - 1 else nc.scalar
-            queue.dma_start(out[:, b * P : (b + 1) * P], result[:])
+            if b < BLOCKS - 1:
+                nc.scalar.copy(result[:], acc[:])
+            else:
+                nc.vector.tensor_copy(result[:], acc[:])
+            nc.sync.dma_start(out[:, b * P : (b + 1) * P], result[:])
 
         zs = [relu(b) for b in range(BLOCKS)]
         for b in range(BLOCKS):

@@ -233,7 +233,7 @@ def tile_picked_zbloom_relu_p_kernel(
                 stop=True,
             )
             result = keep.tile([N, P], F32, name=f"result{b}")
-            if b < BLOCKS - 1:
+            if b < BLOCKS - 2:
                 nc.scalar.copy(result[:], acc[:])
             else:
                 nc.vector.tensor_copy(result[:], acc[:])

@@ -70,7 +70,7 @@ def tile_picked_zbloom_relu_p_kernel(
 
         identity = keep.tile([P, P], F32, name="identity")
         make_identity(nc, identity[:])
-        gate_turned = psum.tile([P, P], F32, name="gate_turned", tag="bank0_0")
+        gate_turned = psum.tile([P, P], F32, name="gate_turned", tag="bank000")
         nc.tensor.transpose(gate_turned[:], gate_rows[:], identity[:])
         gate_cols = keep.tile([P, D * BLOCKS], F32, name="gate_cols")
         nc.scalar.activation(gate_cols[:], gate_turned[:, gate_start:P], ACT.Copy)
@@ -109,36 +109,43 @@ def tile_picked_zbloom_relu_p_kernel(
                 )
                 picked.append(words)
 
-        def weave(engine_copy, grouped, raw, lo, hi):
-            engine_copy(
-                grouped[:, lo:hi, :].rearrange("p (c i) j -> p c j i", i=LINE),
-                raw[:, :, lo:hi].rearrange("p j (c i) -> p c j i", i=LINE),
-            )
+        def dealt(grouped):
+            return grouped.rearrange("p (u m e j) -> p m j u e", u=2, e=2, j=PACK)
+
+        def columns(raw):
+            return raw.rearrange("p j (m u e) -> p m j u e", u=2, e=2)
 
         w1_codes = [keep.tile([P, H], U32, name=f"w1_codes{o}", align_bytes=64) for o in range(PASSES)]
         w1_planes = [keep.tile([P, H], U8, name=f"w1_plane{o}", align_bytes=64) for o in range(PASSES)]
 
         def quantise_w1(o, lo, hi, grouped):
-            nc.vector.quantize_mx(
-                w1_codes[o][:, lo:hi].bitcast(FP8X4), w1_planes[o][:, lo:hi], grouped[:].rearrange("p c j -> p (c j)")
-            )
+            nc.vector.quantize_mx(w1_codes[o][:, lo:hi].bitcast(FP8X4), w1_planes[o][:, lo:hi], grouped)
 
-        grouped_first = keep.tile([P, H, PACK], BF16, name="grouped_first", tag="grouped_then_w2", align_bytes=64)
-        nc.scalar.copy(grouped_first[:], w1_first[:].rearrange("p j c -> p c j"))
-        quantise_w1(0, 0, H, grouped_first)
+        grouped_first = keep.tile([P, H * PACK], BF16, name="grouped_first", tag="grouped_then_w2", align_bytes=64)
+        for h in range(2):
+            nc.scalar.copy(
+                grouped_first[:, h * HALF * PACK : (h + 1) * HALF * PACK].rearrange(
+                    "p (u m e j) -> p m u e j", u=2, e=2, j=PACK
+                ),
+                w1_first[:, :, h * HALF : (h + 1) * HALF].rearrange("p j (m u e) -> p m u e j", u=2, e=2),
+            )
+        quantise_w1(0, 0, H, grouped_first[:])
 
         w1_right = after_cast.tile([P, PACK, HALF], F32, name="w1_right", align_bytes=64, offset=0)
         load_w1(1, w1_right, HALF, H)
         picked_planes.append(after_cast.tile([P, S], U8, name="picked_plane1", align_bytes=64, offset=4608))
         place_scales(1, picked_planes[1])
 
-        grouped_left = keep.tile([P, HALF, PACK], BF16, name="grouped_left", align_bytes=64)
-        grouped_right = keep.tile([P, HALF, PACK], BF16, name="grouped_right", align_bytes=64)
-        weave(nc.scalar.copy, grouped_left, w1_left, 0, HALF)
-        weave(nc.scalar.copy, grouped_right, w1_right, VECTOR_COLUMNS, HALF)
-        quantise_w1(1, 0, HALF, grouped_left)
-        weave(nc.vector.tensor_copy, grouped_right, w1_right, 0, VECTOR_COLUMNS)
-        quantise_w1(1, HALF, H, grouped_right)
+        grouped_left = keep.tile([P, HALF * PACK], BF16, name="grouped_left", tag="left_then_right", align_bytes=64)
+        nc.scalar.copy(dealt(grouped_left[:]), columns(w1_left[:]))
+        quantise_w1(1, 0, HALF, grouped_left[:])
+        QUARTER = HALF // 2
+        right_vector = keep.tile([P, QUARTER * PACK], BF16, name="right_vector", tag="left_then_right", align_bytes=64)
+        right_scalar = keep.tile([P, QUARTER * PACK], BF16, name="right_scalar", align_bytes=64)
+        for u, (copy, grouped) in enumerate(((nc.scalar.copy, right_scalar), (nc.vector.tensor_copy, right_vector))):
+            copy(grouped[:].rearrange("p (m e j) -> p m j e", e=2, j=PACK), columns(w1_right[:])[:, :, :, u, :])
+        quantise_w1(1, HALF, HALF + QUARTER, right_scalar[:])
+        quantise_w1(1, HALF + QUARTER, H, right_vector[:])
 
         w2_codes = keep.tile([P, 2 * N], U8, name="w2_codes", tag="grouped_then_w2", align_bytes=64)
         nc.sync.dma_start(w2_codes[:].bitcast(I32), w2_words[0].bitcast(I32))
@@ -149,63 +156,47 @@ def tile_picked_zbloom_relu_p_kernel(
                 w2_plane[32 * q : 32 * q + 4, :].bitcast(I32), w2_scales[0, 4 * q : 4 * q + 4, :].bitcast(I32)
             )
 
-        y = [[psum.tile([P, H], F32, name=f"y{d}_{b}", tag=f"bank{d}_{b}") for b in range(BLOCKS)] for d in range(D)]
+        y = {
+            (d, h, pair): psum.tile([P, 2, HALF], F32, name=f"y{d}{h}{pair}", tag=f"bank{d}{h}{pair}")
+            for h in range(2)
+            for pair in range(2)
+            for d in range(D)
+        }
+        for o in range(PASSES):
+            for h in range(2):
+                for pair in range(2):
+                    for d in range(D):
+                        for k in range(2):
+                            b = 2 * pair + k
+                            nc.tensor.matmul_mx(
+                                y[d, h, pair][:, k, :],
+                                lhsT=picked[D * o + d][:, b * P : (b + 1) * P].bitcast(FP8X4),
+                                lhsT_scale=picked_planes[o][SHIFT[o] : P, d * V + b * P : d * V + (b + 1) * P],
+                                rhs=w1_codes[o][:, h * HALF : (h + 1) * HALF].bitcast(FP8X4),
+                                rhs_scale=w1_planes[o][:, h * HALF : (h + 1) * HALF],
+                                start=(o == 0 and k == 0),
+                                stop=(o == PASSES - 1 and k == 1),
+                            )
 
-        def first_layer(o, b, d, lo, hi):
-            nc.tensor.matmul_mx(
-                y[d][b][:, lo:hi],
-                lhsT=picked[D * o + d][:, b * P : (b + 1) * P].bitcast(FP8X4),
-                lhsT_scale=picked_planes[o][SHIFT[o] : P, d * V + b * P : d * V + (b + 1) * P],
-                rhs=w1_codes[o][:, lo:hi].bitcast(FP8X4),
-                rhs_scale=w1_planes[o][:, lo:hi],
-                start=(o == 0),
-                stop=(o == PASSES - 1 and hi == H),
-            )
-
-        for b in range(BLOCKS):
-            for d in range(D):
-                first_layer(0, b, d, 0, H)
-        for lo in (0, HALF):
-            for b, d in ((0, 0), (0, 1), (1, 0)):
-                first_layer(1, b, d, lo, lo + HALF)
-        for b in range(1, BLOCKS):
-            if b + 1 < BLOCKS:
-                first_layer(1, b + 1, 0, 0, H)
-            first_layer(1, b, 1, 0, H)
-
-        def pairs_of(bank, u):
-            return bank[:].rearrange("p (m u e) -> p u m e", u=2, e=2)[:, u]
-
+        sums = [keep.tile([P, 2, 2, HALF // 2], BF16, name=f"sums{b}", align_bytes=64) for b in range(BLOCKS)]
+        for h in range(2):
+            for b in range(BLOCKS):
+                gates = [gate_cols[:, d * BLOCKS + b : d * BLOCKS + b + 1] for d in range(D)]
+                scaled = keep.tile([P, HALF], F32, name=f"scaled{h}_{b}")
+                nc.scalar.activation(scaled[:], y[0, h, b // 2][:, b % 2, :], ACT.Copy, scale=gates[0])
+                nc.vector.scalar_tensor_tensor(
+                    sums[b][:, :, h, :],
+                    y[1, h, b // 2][:, b % 2, :].rearrange("p (u c) -> p u c", u=2),
+                    gates[1],
+                    scaled[:].rearrange("p (u c) -> p u c", u=2),
+                    ALU.mult,
+                    ALU.add,
+                )
         turned = []
         for b in range(BLOCKS):
-            gates = [gate_cols[:, d * BLOCKS + b : d * BLOCKS + b + 1] for d in range(D)]
-            scaled = [keep.tile([P, P, 2], F32, name=f"scaled{b}_{u}") for u in range(2)]
-            sums = [keep.tile([P, P, 2], BF16, name=f"sums{b}_{u}", align_bytes=64) for u in range(2)]
-
-            def scale_hash0(u, pairs):
-                nc.scalar.activation(scaled[u][:, pairs], pairs_of(y[0][b], u)[:, pairs], ACT.Copy, scale=gates[0])
-
-            def add_hash(d, u, pairs):
-                nc.vector.scalar_tensor_tensor(
-                    sums[u][:, pairs], pairs_of(y[d][b], u)[:, pairs], gates[d], scaled[u][:, pairs], ALU.mult, ALU.add
-                )
-
-            all_pairs = slice(0, P)
-            if b == 0:
-                pieces = (slice(0, P // 2), slice(P // 2, P))
-                for pairs in pieces:
-                    scale_hash0(0, pairs)
-                nc.vector.tensor_scalar_mul(scaled[1][:], pairs_of(y[1][b], 1), gates[1])
-                for pairs in pieces:
-                    add_hash(1, 0, pairs)
-                add_hash(0, 1, all_pairs)
-            else:
-                for u in range(2):
-                    scale_hash0(u, all_pairs)
-                    add_hash(1, u, all_pairs)
-            bank = psum.tile([P, 2, P], F32, name=f"turned{b}", tag=f"bank0_{b}")
+            bank = psum.tile([P, 2, P], F32, name=f"turned{b}", tag=f"bank{b % 2}0{b // 2}")
             for u in range(2):
-                nc.tensor.transpose(bank[:, u, :], sums[u][:].rearrange("p m e -> p (m e)").bitcast(F32), identity[:])
+                nc.tensor.transpose(bank[:, u, :], sums[b][:, u].rearrange("p h c -> p (h c)").bitcast(F32), identity[:])
             turned.append(bank)
 
         def relu(b):
@@ -222,7 +213,7 @@ def tile_picked_zbloom_relu_p_kernel(
             z_codes = keep.tile([P, P], U32, name=f"z_codes{b}", align_bytes=64)
             z_plane = keep.tile([P, P], U8, name=f"z_plane{b}", align_bytes=64)
             nc.vector.quantize_mx(z_codes[:].bitcast(FP8X4), z_plane[:], z[:])
-            acc = psum.tile([N, P], F32, name=f"acc{b}", tag=f"bank1_{b}")
+            acc = psum.tile([N, P], F32, name=f"acc{b}", tag=f"bank{b % 2}1{b // 2}")
             nc.tensor.matmul_mx(
                 acc[:],
                 lhsT=w2_codes[:].bitcast(FP4X4),

@@ -87,7 +87,7 @@ def tile_picked_zbloom_relu_p_kernel(
                 moved = QUADRANTS
             for q in range(moved):
                 row = STAGE + 16 * o + 4 * q
-                nc.sync.dma_start(
+                (nc.sync if o == 0 else nc.scalar).dma_start(
                     plane[32 * q + SHIFT[o] : 32 * q + SHIFT[o] + 4, :].bitcast(I32),
                     gathered_scales[row : row + 4, :].bitcast(I32),
                 )
@@ -184,14 +184,16 @@ def tile_picked_zbloom_relu_p_kernel(
                 gates = [gate_cols[:, d * BLOCKS + b : d * BLOCKS + b + 1] for d in range(D)]
                 scaled = keep.tile([P, HALF], F32, name=f"scaled{h}_{b}")
                 nc.scalar.activation(scaled[:], y[0, h, b // 2][:, b % 2, :], ACT.Copy, scale=gates[0])
-                nc.vector.scalar_tensor_tensor(
-                    sums[b][:, :, h, :],
-                    y[1, h, b // 2][:, b % 2, :].rearrange("p (u c) -> p u c", u=2),
-                    gates[1],
-                    scaled[:].rearrange("p (u c) -> p u c", u=2),
-                    ALU.mult,
-                    ALU.add,
-                )
+                last = h == 1 and b == BLOCKS - 1
+                for us in (slice(0, 1), slice(1, 2)) if last else (slice(0, 2),):
+                    nc.vector.scalar_tensor_tensor(
+                        sums[b][:, us, h, :],
+                        y[1, h, b // 2][:, b % 2, :].rearrange("p (u c) -> p u c", u=2)[:, us],
+                        gates[1],
+                        scaled[:].rearrange("p (u c) -> p u c", u=2)[:, us],
+                        ALU.mult,
+                        ALU.add,
+                    )
         turned = []
         for b in range(BLOCKS):
             bank = psum.tile([P, 2, P], F32, name=f"turned{b}", tag=f"bank{b % 2}0{b // 2}")

@@ -28,7 +28,7 @@ STAGE = P - 32
 GATE_STEP = 32 * BLOCKS + 1
 SHIFT = (12, 0)
 LINE = 4
-VECTOR_COLUMNS = HALF // 2
+SCALAR_GROUPS = 40
 
 
 def tile_picked_zbloom_relu_p_kernel(
@@ -137,7 +137,11 @@ def tile_picked_zbloom_relu_p_kernel(
         place_scales(1, picked_planes[1])
 
         grouped_left = keep.tile([P, HALF * PACK], BF16, name="grouped_left", tag="left_then_right", align_bytes=64)
-        nc.scalar.copy(dealt(grouped_left[:]), columns(w1_left[:]))
+        nc.scalar.copy(dealt(grouped_left[:])[:, :SCALAR_GROUPS], columns(w1_left[:])[:, :SCALAR_GROUPS])
+        nc.gpsimd.tensor_copy(
+            grouped_left[:].rearrange("p (u m e j) -> p m u e j", u=2, e=2, j=PACK)[:, SCALAR_GROUPS:],
+            w1_left[:].rearrange("p j (m u e) -> p m u e j", u=2, e=2)[:, SCALAR_GROUPS:],
+        )
         quantise_w1(1, 0, HALF, grouped_left[:])
         QUARTER = HALF // 2
         right_vector = keep.tile([P, QUARTER * PACK], BF16, name="right_vector", tag="left_then_right", align_bytes=64)

@@ -29,6 +29,7 @@ GATE_STEP = 32 * BLOCKS + 1
 SHIFT = (12, 0)
 LINE = 4
 SCALAR_GROUPS = 40
+VECTOR_GROUPS = 48
 
 
 def tile_picked_zbloom_relu_p_kernel(
@@ -101,13 +102,9 @@ def tile_picked_zbloom_relu_p_kernel(
 
         picked = []
         for o in range(PASSES):
-            for d in range(D):
-                words = keep.tile([P, V], U32, name=f"picked{o}_{d}", align_bytes=64)
-                nc.vector.tensor_copy(
-                    words[:],
-                    table_words[o][:].bitcast(U32).indirect(offsets[:, d * V // 16 : (d + 1) * V // 16]),
-                )
-                picked.append(words)
+            words = keep.tile([P, S], U32, name=f"picked{o}", align_bytes=64)
+            nc.vector.tensor_copy(words[:], table_words[o][:].bitcast(U32).indirect(offsets[:]))
+            picked.append(words)
 
         def dealt(grouped):
             return grouped.rearrange("p (u m e j) -> p m j u e", u=2, e=2, j=PACK)
@@ -124,10 +121,8 @@ def tile_picked_zbloom_relu_p_kernel(
         grouped_first = keep.tile([P, H * PACK], BF16, name="grouped_first", tag="grouped_then_w2", align_bytes=64)
         for h in range(2):
             nc.scalar.copy(
-                grouped_first[:, h * HALF * PACK : (h + 1) * HALF * PACK].rearrange(
-                    "p (u m e j) -> p m u e j", u=2, e=2, j=PACK
-                ),
-                w1_first[:, :, h * HALF : (h + 1) * HALF].rearrange("p j (m u e) -> p m u e j", u=2, e=2),
+                dealt(grouped_first[:, h * HALF * PACK : (h + 1) * HALF * PACK]),
+                columns(w1_first[:, :, h * HALF : (h + 1) * HALF]),
             )
         quantise_w1(0, 0, H, grouped_first[:])
 
@@ -146,8 +141,15 @@ def tile_picked_zbloom_relu_p_kernel(
         QUARTER = HALF // 2
         right_vector = keep.tile([P, QUARTER * PACK], BF16, name="right_vector", tag="left_then_right", align_bytes=64)
         right_scalar = keep.tile([P, QUARTER * PACK], BF16, name="right_scalar", align_bytes=64)
-        for u, (copy, grouped) in enumerate(((nc.scalar.copy, right_scalar), (nc.vector.tensor_copy, right_vector))):
-            copy(grouped[:].rearrange("p (m e j) -> p m j e", e=2, j=PACK), columns(w1_right[:])[:, :, :, u, :])
+        for copy, grouped, u, groups in (
+            (nc.scalar.copy, right_scalar, 0, slice(0, 64)),
+            (nc.vector.tensor_copy, right_vector, 1, slice(0, VECTOR_GROUPS)),
+            (nc.scalar.copy, right_vector, 1, slice(VECTOR_GROUPS, 64)),
+        ):
+            copy(
+                grouped[:].rearrange("p (m e j) -> p m j e", e=2, j=PACK)[:, groups],
+                columns(w1_right[:])[:, groups, :, u, :],
+            )
         quantise_w1(1, HALF, HALF + QUARTER, right_scalar[:])
         quantise_w1(1, HALF + QUARTER, H, right_vector[:])
 
@@ -174,7 +176,7 @@ def tile_picked_zbloom_relu_p_kernel(
                             b = 2 * pair + k
                             nc.tensor.matmul_mx(
                                 y[d, h, pair][:, k, :],
-                                lhsT=picked[D * o + d][:, b * P : (b + 1) * P].bitcast(FP8X4),
+                                lhsT=picked[o][:, d * V + b * P : d * V + (b + 1) * P].bitcast(FP8X4),
                                 lhsT_scale=picked_planes[o][SHIFT[o] : P, d * V + b * P : d * V + (b + 1) * P],
                                 rhs=w1_codes[o][:, h * HALF : (h + 1) * HALF].bitcast(FP8X4),
                                 rhs_scale=w1_planes[o][:, h * HALF : (h + 1) * HALF],
@@ -188,16 +190,14 @@ def tile_picked_zbloom_relu_p_kernel(
                 gates = [gate_cols[:, d * BLOCKS + b : d * BLOCKS + b + 1] for d in range(D)]
                 scaled = keep.tile([P, HALF], F32, name=f"scaled{h}_{b}")
                 nc.scalar.activation(scaled[:], y[0, h, b // 2][:, b % 2, :], ACT.Copy, scale=gates[0])
-                last = h == 1 and b == BLOCKS - 1
-                for us in (slice(0, 1), slice(1, 2)) if last else (slice(0, 2),):
-                    nc.vector.scalar_tensor_tensor(
-                        sums[b][:, us, h, :],
-                        y[1, h, b // 2][:, b % 2, :].rearrange("p (u c) -> p u c", u=2)[:, us],
-                        gates[1],
-                        scaled[:].rearrange("p (u c) -> p u c", u=2)[:, us],
-                        ALU.mult,
-                        ALU.add,
-                    )
+                nc.vector.scalar_tensor_tensor(
+                    sums[b][:, :, h, :],
+                    y[1, h, b // 2][:, b % 2, :].rearrange("p (u c) -> p u c", u=2),
+                    gates[1],
+                    scaled[:].rearrange("p (u c) -> p u c", u=2),
+                    ALU.mult,
+                    ALU.add,
+                )
         turned = []
         for b in range(BLOCKS):
             bank = psum.tile([P, 2, P], F32, name=f"turned{b}", tag=f"bank{b % 2}0{b // 2}")
@@ -236,6 +236,7 @@ def tile_picked_zbloom_relu_p_kernel(
                 nc.vector.tensor_copy(result[:], acc[:])
             nc.sync.dma_start(out[:, b * P : (b + 1) * P], result[:])
 
-        zs = [relu(b) for b in range(BLOCKS)]
-        for b in range(BLOCKS):
-            second_layer(b, zs[b])
+        for pair in range(2):
+            zs = [relu(b) for b in (2 * pair, 2 * pair + 1)]
+            for k in range(2):
+                second_layer(2 * pair + k, zs[k])

@@ -29,7 +29,7 @@ GATE_STEP = 32 * BLOCKS + 1
 SHIFT = (12, 0)
 LINE = 4
 SCALAR_GROUPS = 40
-VECTOR_GROUPS = 48
+LAST_SCALAR_GROUPS = 44
 
 
 def tile_picked_zbloom_relu_p_kernel(
@@ -142,9 +142,9 @@ def tile_picked_zbloom_relu_p_kernel(
         right_vector = keep.tile([P, QUARTER * PACK], BF16, name="right_vector", tag="left_then_right", align_bytes=64)
         right_scalar = keep.tile([P, QUARTER * PACK], BF16, name="right_scalar", align_bytes=64)
         for copy, grouped, u, groups in (
-            (nc.scalar.copy, right_scalar, 0, slice(0, 64)),
-            (nc.vector.tensor_copy, right_vector, 1, slice(0, VECTOR_GROUPS)),
-            (nc.scalar.copy, right_vector, 1, slice(VECTOR_GROUPS, 64)),
+            (nc.scalar.copy, right_scalar, 0, slice(0, LAST_SCALAR_GROUPS)),
+            (nc.vector.tensor_copy, right_scalar, 0, slice(LAST_SCALAR_GROUPS, 64)),
+            (nc.vector.tensor_copy, right_vector, 1, slice(0, 64)),
         ):
             copy(
                 grouped[:].rearrange("p (m e j) -> p m j e", e=2, j=PACK)[:, groups],

@@ -65,7 +65,7 @@ def tile_picked_zbloom_relu_p_kernel(
         nc.vector.memset(gate_rows[STAGE:gate_start, :], 0.0)
 
         x_rows = [x_words[o].rearrange("p n t -> p (n t)").bitcast(I32) for o in range(PASSES)]
-        table_words = [keep.tile([P, T], I32, name="table_words0", align_bytes=64)]
+        table_words = [keep.tile([P, T], I32, name="table_words0", tag="table_then_plane", align_bytes=64)]
         nc.sync.dma_start(table_words[0][:], x_rows[0])
         load_w1(0, w1_first, 0, H)
 
@@ -88,7 +88,7 @@ def tile_picked_zbloom_relu_p_kernel(
                 moved = QUADRANTS
             for q in range(moved):
                 row = STAGE + 16 * o + 4 * q
-                (nc.sync if o == 0 else nc.scalar).dma_start(
+                nc.sync.dma_start(
                     plane[32 * q + SHIFT[o] : 32 * q + SHIFT[o] + 4, :].bitcast(I32),
                     gathered_scales[row : row + 4, :].bitcast(I32),
                 )
@@ -128,7 +128,7 @@ def tile_picked_zbloom_relu_p_kernel(
 
         w1_right = after_cast.tile([P, PACK, HALF], F32, name="w1_right", align_bytes=64, offset=0)
         load_w1(1, w1_right, HALF, H)
-        picked_planes.append(after_cast.tile([P, S], U8, name="picked_plane1", align_bytes=64, offset=4608))
+        picked_planes.append(keep.tile([P, S], U8, name="picked_plane1", tag="table_then_plane", align_bytes=64))
         place_scales(1, picked_planes[1])
 
         grouped_left = keep.tile([P, HALF * PACK], BF16, name="grouped_left", tag="left_then_right", align_bytes=64)

@@ -137,7 +137,8 @@ def tile_picked_zbloom_relu_p_kernel(
             grouped_left[:].rearrange("p (u m e j) -> p m u e j", u=2, e=2, j=PACK)[:, SCALAR_GROUPS:],
             w1_left[:].rearrange("p j (m u e) -> p m u e j", u=2, e=2)[:, SCALAR_GROUPS:],
         )
-        quantise_w1(1, 0, HALF, grouped_left[:])
+        for u in range(2):
+            quantise_w1(1, u * P, (u + 1) * P, grouped_left[:, u * P * PACK : (u + 1) * P * PACK])
         QUARTER = HALF // 2
         right_vector = keep.tile([P, QUARTER * PACK], BF16, name="right_vector", tag="left_then_right", align_bytes=64)
         right_scalar = keep.tile([P, QUARTER * PACK], BF16, name="right_scalar", align_bytes=64)
@@ -168,21 +169,28 @@ def tile_picked_zbloom_relu_p_kernel(
             for pair in range(2)
             for d in range(D)
         }
+        def first_layer(o, h, pair, d, lo, hi):
+            for k in range(2):
+                b = 2 * pair + k
+                nc.tensor.matmul_mx(
+                    y[d, h, pair][:, k, lo:hi],
+                    lhsT=picked[o][:, d * V + b * P : d * V + (b + 1) * P].bitcast(FP8X4),
+                    lhsT_scale=picked_planes[o][SHIFT[o] : P, d * V + b * P : d * V + (b + 1) * P],
+                    rhs=w1_codes[o][:, h * HALF + lo : h * HALF + hi].bitcast(FP8X4),
+                    rhs_scale=w1_planes[o][:, h * HALF + lo : h * HALF + hi],
+                    start=(o == 0 and k == 0),
+                    stop=(o == PASSES - 1 and k == 1 and hi == HALF),
+                )
+
         for o in range(PASSES):
             for h in range(2):
                 for pair in range(2):
                     for d in range(D):
-                        for k in range(2):
-                            b = 2 * pair + k
-                            nc.tensor.matmul_mx(
-                                y[d, h, pair][:, k, :],
-                                lhsT=picked[o][:, d * V + b * P : d * V + (b + 1) * P].bitcast(FP8X4),
-                                lhsT_scale=picked_planes[o][SHIFT[o] : P, d * V + b * P : d * V + (b + 1) * P],
-                                rhs=w1_codes[o][:, h * HALF : (h + 1) * HALF].bitcast(FP8X4),
-                                rhs_scale=w1_planes[o][:, h * HALF : (h + 1) * HALF],
-                                start=(o == 0 and k == 0),
-                                stop=(o == PASSES - 1 and k == 1),
-                            )
+                        if (o, h, pair, d) == (1, 0, 0, 0):
+                            first_layer(o, h, pair, d, 0, P)
+                            first_layer(o, h, pair, d, P, HALF)
+                        else:
+                            first_layer(o, h, pair, d, 0, HALF)
 
         sums = [keep.tile([P, 2, 2, HALF // 2], BF16, name=f"sums{b}", align_bytes=64) for b in range(BLOCKS)]
         for h in range(2):

from contextlib import ExitStack

import concourse.mybir as mybir
from concourse.masks import make_identity

K, T, S, D, V, H, N = 1024, 4096, 1024, 2, 512, 512, 128
FLOPS = 2 * K * H * S + 2 * H * N * V
BYTES = K * T + K * T // 32 + 4 * K * H + H * N // 2 + H * N // 32 + 4 * D * V + 2 * 128 * S // 16 + 4 * N * V

F32 = mybir.dt.float32
BF16 = mybir.dt.bfloat16
I32 = mybir.dt.int32
U32 = mybir.dt.uint32
U16 = mybir.dt.uint16
U8 = mybir.dt.uint8
FP8X4 = mybir.dt.float8_e4m3fn_x4
FP4X4 = mybir.dt.float4_e2m1fn_x4
ACT = mybir.ActivationFunctionType
ALU = mybir.AluOpType

P = 128
PACK = 4
PASSES = K // (P * PACK)
BLOCKS = V // P
HALF = H // 2
QUADRANTS = 4
STAGE = P - 32
GATE_STEP = 32 * BLOCKS + 1
SHIFT = (12, 0)
LINE = 4
SCALAR_GROUPS = 40
LAST_SCALAR_GROUPS = 44


def tile_picked_zbloom_relu_p_kernel(
    tc, x_words, x_scales, w1, w2_words, w2_scales, gate, offs, out
):
    nc = tc.nc
    with ExitStack() as ctx:
        keep = ctx.enter_context(tc.tile_pool(name="keep", bufs=1))
        after_scales = ctx.enter_context(tc.tile_pool(name="after_scales", bufs=1))
        after_cast = ctx.enter_context(tc.tile_pool(name="after_cast", bufs=1))
        psum = ctx.enter_context(tc.psum_pool(name="psum", bufs=1))

        table_scales = after_scales.tile([P, T], U8, name="table_scales", align_bytes=64, offset=2048)
        nc.sync.dma_start(
            table_scales[STAGE:P, :].bitcast(I32), x_scales.rearrange("o q n -> (o q) n").bitcast(I32)
        )
        nc.vector.memset(table_scales[0:STAGE, :].bitcast(I32), 0)

        offsets = keep.tile([P, S // 16], U16, name="offsets")
        nc.sync.dma_start(offsets[:], offs)

        def load_w1(o, raw, lo, hi):
            rows = w1[P * PACK * o : P * PACK * (o + 1), lo:hi]
            nc.sync.dma_start(raw[:], rows.rearrange("(p j) c -> p j c", j=PACK))

        w1_first = after_cast.tile([P, PACK, H], F32, name="w1_first", align_bytes=64, offset=0)

        gate_start = P - D * BLOCKS
        gate_rows = keep.tile([P, P], F32, name="gate_rows")
        gate_pieces = gate.rearrange("d r (b p) -> (d r b) p", p=P)
        nc.scalar.dma_start(gate_rows[gate_start:P, :], gate_pieces[0 : D * P * BLOCKS : GATE_STEP])
        nc.vector.memset(gate_rows[0:STAGE, :], 0.0)
        nc.vector.memset(gate_rows[STAGE:gate_start, :], 0.0)

        x_rows = [x_words[o].rearrange("p n t -> p (n t)").bitcast(I32) for o in range(PASSES)]
        table_words = [keep.tile([P, T], I32, name="table_words0", tag="table_then_plane", align_bytes=64)]
        nc.sync.dma_start(table_words[0][:], x_rows[0])
        load_w1(0, w1_first, 0, H)

        identity = keep.tile([P, P], F32, name="identity")
        make_identity(nc, identity[:])
        gate_turned = psum.tile([P, P], F32, name="gate_turned", tag="bank000")
        nc.tensor.transpose(gate_turned[:], gate_rows[:], identity[:])
        gate_cols = keep.tile([P, D * BLOCKS], F32, name="gate_cols")
        nc.scalar.activation(gate_cols[:], gate_turned[:, gate_start:P], ACT.Copy)

        gathered_scales = keep.tile([P, S], U8, name="gathered_scales", align_bytes=64)
        nc.vector.tensor_copy(gathered_scales[:], table_scales[:].indirect(offsets[:]))

        def place_scales(o, plane):
            if o == 0:
                nc.vector.tensor_copy(plane[:].bitcast(I32), gathered_scales[:].bitcast(I32))
                moved = QUADRANTS - 1
            else:
                nc.vector.memset(plane[:].bitcast(I32), 0)
                moved = QUADRANTS
            for q in range(moved):
                row = STAGE + 16 * o + 4 * q
                nc.sync.dma_start(
                    plane[32 * q + SHIFT[o] : 32 * q + SHIFT[o] + 4, :].bitcast(I32),
                    gathered_scales[row : row + 4, :].bitcast(I32),
                )

        table_words.append(after_scales.tile([P, T], I32, name="table_words1", align_bytes=64, offset=4096))
        picked_planes = [keep.tile([P, S], U8, name="picked_plane0", align_bytes=64)]
        place_scales(0, picked_planes[0])
        nc.sync.dma_start(table_words[1][:], x_rows[1])
        w1_left = after_scales.tile([P, PACK, HALF], F32, name="w1_left", align_bytes=64, offset=0)
        load_w1(1, w1_left, 0, HALF)

        picked = []
        for o in range(PASSES):
            words = keep.tile([P, S], U32, name=f"picked{o}", align_bytes=64)
            nc.vector.tensor_copy(words[:], table_words[o][:].bitcast(U32).indirect(offsets[:]))
            picked.append(words)

        def dealt(grouped):
            return grouped.rearrange("p (u m e j) -> p m j u e", u=2, e=2, j=PACK)

        def columns(raw):
            return raw.rearrange("p j (m u e) -> p m j u e", u=2, e=2)

        w1_codes = [keep.tile([P, H], U32, name=f"w1_codes{o}", align_bytes=64) for o in range(PASSES)]
        w1_planes = [keep.tile([P, H], U8, name=f"w1_plane{o}", align_bytes=64) for o in range(PASSES)]

        def quantise_w1(o, lo, hi, grouped):
            nc.vector.quantize_mx(w1_codes[o][:, lo:hi].bitcast(FP8X4), w1_planes[o][:, lo:hi], grouped)

        grouped_first = keep.tile([P, H * PACK], BF16, name="grouped_first", tag="grouped_then_w2", align_bytes=64)
        for h in range(2):
            nc.scalar.copy(
                dealt(grouped_first[:, h * HALF * PACK : (h + 1) * HALF * PACK]),
                columns(w1_first[:, :, h * HALF : (h + 1) * HALF]),
            )
        quantise_w1(0, 0, H, grouped_first[:])

        w1_right = after_cast.tile([P, PACK, HALF], F32, name="w1_right", align_bytes=64, offset=0)
        load_w1(1, w1_right, HALF, H)
        picked_planes.append(keep.tile([P, S], U8, name="picked_plane1", tag="table_then_plane", align_bytes=64))
        place_scales(1, picked_planes[1])

        grouped_left = keep.tile([P, HALF * PACK], BF16, name="grouped_left", tag="left_then_right", align_bytes=64)
        nc.scalar.copy(dealt(grouped_left[:])[:, :SCALAR_GROUPS], columns(w1_left[:])[:, :SCALAR_GROUPS])
        nc.gpsimd.tensor_copy(
            grouped_left[:].rearrange("p (u m e j) -> p m u e j", u=2, e=2, j=PACK)[:, SCALAR_GROUPS:],
            w1_left[:].rearrange("p j (m u e) -> p m u e j", u=2, e=2)[:, SCALAR_GROUPS:],
        )
        for u in range(2):
            quantise_w1(1, u * P, (u + 1) * P, grouped_left[:, u * P * PACK : (u + 1) * P * PACK])
        QUARTER = HALF // 2
        right_vector = keep.tile([P, QUARTER * PACK], BF16, name="right_vector", tag="left_then_right", align_bytes=64)
        right_scalar = keep.tile([P, QUARTER * PACK], BF16, name="right_scalar", align_bytes=64)
        for copy, grouped, u, groups in (
            (nc.scalar.copy, right_scalar, 0, slice(0, LAST_SCALAR_GROUPS)),
            (nc.vector.tensor_copy, right_scalar, 0, slice(LAST_SCALAR_GROUPS, 64)),
            (nc.vector.tensor_copy, right_vector, 1, slice(0, 64)),
        ):
            copy(
                grouped[:].rearrange("p (m e j) -> p m j e", e=2, j=PACK)[:, groups],
                columns(w1_right[:])[:, groups, :, u, :],
            )
        quantise_w1(1, HALF, HALF + QUARTER, right_scalar[:])
        quantise_w1(1, HALF + QUARTER, H, right_vector[:])

        w2_codes = keep.tile([P, 2 * N], U8, name="w2_codes", tag="grouped_then_w2", align_bytes=64)
        nc.sync.dma_start(w2_codes[:].bitcast(I32), w2_words[0].bitcast(I32))
        w2_plane = after_cast.tile([P, N], U8, name="w2_plane", align_bytes=64, offset=4096)
        nc.vector.memset(w2_plane[:].bitcast(I32), 0)
        for q in range(QUADRANTS):
            nc.sync.dma_start(
                w2_plane[32 * q : 32 * q + 4, :].bitcast(I32), w2_scales[0, 4 * q : 4 * q + 4, :].bitcast(I32)
            )

        y = {
            (d, h, pair): psum.tile([P, 2, HALF], F32, name=f"y{d}{h}{pair}", tag=f"bank{d}{h}{pair}")
            for h in range(2)
            for pair in range(2)
            for d in range(D)
        }
        def first_layer(o, h, pair, d, lo, hi):
            for k in range(2):
                b = 2 * pair + k
                nc.tensor.matmul_mx(
                    y[d, h, pair][:, k, lo:hi],
                    lhsT=picked[o][:, d * V + b * P : d * V + (b + 1) * P].bitcast(FP8X4),
                    lhsT_scale=picked_planes[o][SHIFT[o] : P, d * V + b * P : d * V + (b + 1) * P],
                    rhs=w1_codes[o][:, h * HALF + lo : h * HALF + hi].bitcast(FP8X4),
                    rhs_scale=w1_planes[o][:, h * HALF + lo : h * HALF + hi],
                    start=(o == 0 and k == 0),
                    stop=(o == PASSES - 1 and k == 1 and hi == HALF),
                )

        for o in range(PASSES):
            for h in range(2):
                for pair in range(2):
                    for d in range(D):
                        if (o, h, pair, d) == (1, 0, 0, 0):
                            first_layer(o, h, pair, d, 0, P)
                            first_layer(o, h, pair, d, P, HALF)
                        else:
                            first_layer(o, h, pair, d, 0, HALF)

        sums = [keep.tile([P, 2, 2, HALF // 2], BF16, name=f"sums{b}", align_bytes=64) for b in range(BLOCKS)]
        for h in range(2):
            for b in range(BLOCKS):
                gates = [gate_cols[:, d * BLOCKS + b : d * BLOCKS + b + 1] for d in range(D)]
                scaled = keep.tile([P, HALF], F32, name=f"scaled{h}_{b}")
                nc.scalar.activation(scaled[:], y[0, h, b // 2][:, b % 2, :], ACT.Copy, scale=gates[0])
                nc.vector.scalar_tensor_tensor(
                    sums[b][:, :, h, :],
                    y[1, h, b // 2][:, b % 2, :].rearrange("p (u c) -> p u c", u=2),
                    gates[1],
                    scaled[:].rearrange("p (u c) -> p u c", u=2),
                    ALU.mult,
                    ALU.add,
                )
        turned = []
        for b in range(BLOCKS):
            bank = psum.tile([P, 2, P], F32, name=f"turned{b}", tag=f"bank{b % 2}0{b // 2}")
            for u in range(2):
                nc.tensor.transpose(bank[:, u, :], sums[b][:, u].rearrange("p h c -> p (h c)").bitcast(F32), identity[:])
            turned.append(bank)

        def relu(b):
            z = keep.tile([P, P * PACK], BF16, name=f"z{b}", align_bytes=64)
            woven = z[:].rearrange("p (v u e) -> p v u e", u=2, e=2)
            halves = turned[b][:].rearrange("p u v -> p (u v)").bitcast(BF16).rearrange("p (u v e) -> p v u e", u=2, e=2)
            if b % 2 == 0:
                nc.scalar.activation(woven, halves, ACT.Relu)
            else:
                nc.vector.tensor_scalar_max(woven, halves, 0.0)
            return z

        def second_layer(b, z):
            z_codes = keep.tile([P, P], U32, name=f"z_codes{b}", align_bytes=64)
            z_plane = keep.tile([P, P], U8, name=f"z_plane{b}", align_bytes=64)
            nc.vector.quantize_mx(z_codes[:].bitcast(FP8X4), z_plane[:], z[:])
            acc = psum.tile([N, P], F32, name=f"acc{b}", tag=f"bank{b % 2}1{b // 2}")
            nc.tensor.matmul_mx(
                acc[:],
                lhsT=w2_codes[:].bitcast(FP4X4),
                lhsT_scale=w2_plane[:],
                rhs=z_codes[:].bitcast(FP8X4),
                rhs_scale=z_plane[:],
                start=True,
                stop=True,
            )
            result = keep.tile([N, P], F32, name=f"result{b}")
            if b < BLOCKS - 2:
                nc.scalar.copy(result[:], acc[:])
            else:
                nc.vector.tensor_copy(result[:], acc[:])
            nc.sync.dma_start(out[:, b * P : (b + 1) * P], result[:])

        for pair in range(2):
            zs = [relu(b) for b in (2 * pair, 2 * pair + 1)]
            for k in range(2):
                second_layer(2 * pair + k, zs[k])
